import numpy as np
import ml_dtypes


def mxq(x, axis, fmt="e4m3"):
    dtype, down = {"e4m3": (ml_dtypes.float8_e4m3fn, 7), "e5m2": (ml_dtypes.float8_e5m2, 14)}[fmt]
    v = np.moveaxis(np.asarray(x, np.float32).astype(ml_dtypes.bfloat16).astype(np.float64), axis, -1)
    blocks = v.reshape(v.shape[:-1] + (-1, 32))
    amax = np.abs(blocks).max(-1, keepdims=True)
    byte = np.maximum(np.where(amax > 0, np.frexp(amax)[1] - 1 + 127, 0) - down, 1)
    scale = np.exp2(byte - 127.0)
    codes = (blocks / scale).astype(np.float32).astype(dtype).astype(np.float64)
    return np.moveaxis((codes * scale).reshape(v.shape), -1, axis)


WIDE = False


def mx_kscale(k):
    if not WIDE:
        return np.ones(k)
    levels = np.array([10, -10, 5, -5, 0])
    if k % 512:
        return np.exp2(np.random.permutation(np.resize(levels, k // 32))).repeat(32)
    a = np.empty((k // 512, 16))
    for p in range(k // 512):
        a[p, :8] = np.random.permutation(np.resize(levels, 8))
        for g in range(8):
            far = levels[np.abs(levels - a[p, g]) >= 10]
            a[p, g + 8] = far[np.random.randint(len(far))]
    return np.exp2(a.ravel()).repeat(32)


def f64(x):
    return np.asarray(x).astype(np.float64)


def striped(idx):
    return np.tile(idx.reshape(-1, 16).T, (8, 1)).astype(np.uint16)


def unstriped(offs):
    return offs[:16].T.reshape(-1).astype(np.int64)


E2M1 = np.array([0.0, 0.5, 1.0, 1.5, 2.0, 3.0, 4.0, 6.0, -0.0, -0.5, -1.0, -1.5, -2.0, -3.0, -4.0, -6.0])


def pack_weight(w, fmt):
    k, n = w.shape
    w = f64(np.asarray(w, np.float32).astype(ml_dtypes.bfloat16)).reshape(k // 32, 32, n)
    amax = np.abs(w).max(1)
    if fmt == "e4m3":
        byte = np.frexp(amax)[1] - 1 + 127 - 7
    else:
        mant, ex = np.frexp(amax / 6.0)
        byte = np.where(mant > 0.5, ex, ex - 1) + 127
    byte = np.clip(np.where(amax > 0, byte, 1), 1, 254)
    scaled = (w * np.exp2(127.0 - byte)[:, None, :]).reshape(k, n).astype(np.float32)
    by_word = np.ascontiguousarray(scaled.reshape(k // 512, 128, 4, n).transpose(0, 1, 3, 2))
    if fmt == "e4m3":
        words = by_word.astype(ml_dtypes.float8_e4m3fn).view(np.uint8)
    else:
        c = by_word.astype(ml_dtypes.float4_e2m1fn).view(np.uint8) & 0xF
        words = (c[..., 0::2] | (c[..., 1::2] << 4)).reshape(k // 512, 128, 2 * n)
    return np.ascontiguousarray(words), np.ascontiguousarray(byte.astype(np.uint8).reshape(k // 512, 16, n))


def unpack_weight(words, scales, fmt):
    g, _, n = scales.shape
    words = np.ascontiguousarray(words).reshape(g, 128, n, -1)
    if fmt == "e4m3":
        vals = words.view(ml_dtypes.float8_e4m3fn).astype(np.float64)
    else:
        nib = np.empty((g, 128, n, 4), np.uint8)
        nib[..., 0::2] = words & 0xF
        nib[..., 1::2] = words >> 4
        vals = E2M1[nib]
    vals = vals * np.repeat(np.exp2(scales.astype(np.float64) - 127.0), 8, axis=1)[..., None]
    return vals.transpose(0, 1, 3, 2).reshape(g * 512, n)


def gelu(v):
    return 0.5 * v * (1.0 + np.tanh(np.sqrt(2.0 / np.pi) * (v + 0.044715 * v**3)))


def bf(x):
    return np.asarray(x, np.float32).astype(ml_dtypes.bfloat16)


def planes(Y):
    n, m = Y.shape
    b = f64(bf(Y)).reshape(n // 32, 32, m)
    amax = np.abs(b).max(1)
    byte = np.clip(np.where(amax > 0, np.frexp(amax)[1] - 1 + 127 - 7, 1), 1, 254)
    codes = (b * np.exp2(127.0 - byte)[:, None, :]).reshape(n, m).astype(np.float32).astype(ml_dtypes.float8_e4m3fn).view(np.uint8)
    words = codes.reshape(n // 512, 128, 4, m).transpose(0, 1, 3, 2)
    return np.ascontiguousarray(words), np.ascontiguousarray(byte.astype(np.uint8).reshape(n // 512, 16, m))


K, K2, H, N, T, TC, S, T2, P = 1024, 512, 1024, 512, 2048, 1024, 512, 2048, 1024


def setup_inputs():
    n = np.random.standard_normal
    s, s2, u = mx_kscale(K)[:, None], mx_kscale(K2)[:, None], mx_kscale(H)[:, None]
    e = np.exp(0.8 * n(N))
    perm = np.random.permutation(T2)
    d = {}
    d["tab_words"], d["tab_scales"] = pack_weight(n((K, T)) * s, "e4m3")
    d["tab2_words"], d["tab2_scales"] = pack_weight(n((K2, TC)) * s2, "e4m3")
    d["offs"] = striped(np.random.permutation(T)[:S])
    d["offs2"] = striped(np.random.permutation(TC)[:S])
    d["offs3"] = striped(perm[:S])
    d["offs4"] = striped(perm[S:2 * S])
    d["offs5"] = striped(np.random.permutation(T2)[:P])
    d["w1"] = (1.4 * n((K, H)) / s / K ** 0.5).astype(np.float32)
    d["g1"] = (1.3 * np.exp(0.3 * n(H)) * u[:, 0]).astype(np.float32)
    d["w2_words"], d["w2_scales"] = pack_weight(1.4 * n((K2, H)) / s2 * u.T ** 2 / K2 ** 0.5, "e2m1")
    d["page0"] = (n((H, T2)) * u).astype(np.float32)
    d["wg1"] = np.exp(0.3 * n((128, S))).astype(np.float32)
    d["wg2"] = np.exp(0.3 * n((128, S))).astype(np.float32)
    d["rg"] = np.exp(0.4 * n(H)).astype(np.float32)
    d["w3"] = (n((H, N)) * e / u / H ** 0.5).astype(np.float32)
    d["w4_words"], d["w4_scales"] = pack_weight(n((H, N)) / u / H ** 0.5, "e2m1")
    d["w5_words"], d["w5_scales"] = pack_weight(n((H, N)) * e / u / H ** 0.5, "e4m3")
    return d


def reference(tab_words, tab_scales, tab2_words, tab2_scales, offs, offs2, offs3, offs4, offs5,
              w1, g1, w2_words, w2_scales, page0, wg1, wg2, rg, w3, w4_words, w4_scales, w5_words, w5_scales):
    v = unpack_weight(tab_words, tab_scales, "e4m3")[:, unstriped(offs)]
    v2 = unpack_weight(tab2_words, tab2_scales, "e4m3")[:, unstriped(offs2)]
    h1 = np.tanh(mxq(f64(w1), 0, "e4m3").T @ v) * f64(g1)[:, None]
    h2 = np.sqrt(np.abs(unpack_weight(w2_words, w2_scales, "e2m1").T @ v2))
    page = f64(page0).copy()
    page[:, unstriped(offs3)] = np.tile(f64(wg1), (H // 128, 1)) * h1
    page[:, unstriped(offs4)] = np.tile(f64(wg2), (H // 128, 1)) * h2
    x = mxq(page[:, unstriped(offs5)] * f64(rg)[:, None], 0, "e4m3")
    y3 = mxq(f64(w3), 0, "e4m3").T @ x
    y4 = unpack_weight(w4_words, w4_scales, "e2m1").T @ x
    y5 = unpack_weight(w5_words, w5_scales, "e4m3").T @ x
    y = y3 * y4 + y5
    words, scales = planes(y)
    return y, words, scales

@@ -1,0 +1,323 @@
+from contextlib import ExitStack
+
+import concourse.mybir as mybir
+from concourse.masks import make_identity
+
+F32 = mybir.dt.float32
+BF16 = mybir.dt.bfloat16
+I32 = mybir.dt.int32
+U32 = mybir.dt.uint32
+U16 = mybir.dt.uint16
+U8 = mybir.dt.uint8
+FP8X4 = mybir.dt.float8_e4m3fn_x4
+FP4X4 = mybir.dt.float4_e2m1fn_x4
+ACT = mybir.ActivationFunctionType
+MULT = mybir.AluOpType.mult
+ADD = mybir.AluOpType.add
+
+K, K2, H, N, T, TC, S, T2, PICK = 1024, 512, 1024, 512, 2048, 1024, 512, 2048, 1024
+FLOPS = 2 * (K * H * S + K2 * H * S + 3 * H * N * PICK)
+
+P = 128
+PACK = 4
+PASS = P * PACK
+CHUNK = 256
+
+
+def tile_list_electrolyser_slot_features_kernel(
+    tc, tab_words, tab_scales, tab2_words, tab2_scales, offs, offs2, offs3, offs4, offs5,
+    w1, g1, w2_words, w2_scales, page0, wg1, wg2, rg, w3, w4_words, w4_scales, w5_words, w5_scales,
+    out_0, out_1, out_2,
+):
+    nc = tc.nc
+    with ExitStack() as ctx:
+        lists = ctx.enter_context(tc.tile_pool(name="lists", bufs=1))
+        keep = ctx.enter_context(tc.tile_pool(name="keep", bufs=1))
+        ring = ctx.enter_context(tc.tile_pool(name="ring", bufs=2))
+        psum = ctx.enter_context(tc.psum_pool(name="psum", bufs=1))
+
+        def kept(name, shape, dtype):
+            return keep.tile(shape, dtype, name=name, align_bytes=64)
+
+        def load_list(name, src):
+            tile = lists.tile(list(src.shape), U16, name=name)
+            nc.sync.dma_start(tile[:], src)
+            return tile
+
+        def zeroed_plane(name, width, engine):
+            plane = kept(name, [P, width], U8)
+            engine.memset(plane[:].bitcast(I32), 0)
+            return plane
+
+        def in_slot(slot, name, shape, dtype):
+            return ring.tile(shape, dtype, name=name, tag=slot, bufs=1, align_bytes=64)
+
+        def f512(name):
+            return ring.tile([P, S], F32, name=name, tag="f512", bufs=12, align_bytes=64)
+
+        def bank_a(name):
+            return psum.tile([P, S], F32, name=name, tag="bank_a", bufs=2)
+
+        def bank_b(name):
+            return psum.tile([P, S], F32, name=name, tag="bank_b", bufs=6)
+
+        tab2_s = zeroed_plane("tab2_s", TC, nc.gpsimd)
+        w2_s = zeroed_plane("w2_s", H, nc.gpsimd)
+        tab_s = zeroed_plane("tab_s", T, nc.vector)
+        w45_s_raw = zeroed_plane("w45_s_raw", 2 * N, nc.vector)
+
+        ident = kept("ident", [P, P], F32)
+        make_identity(nc, ident[:])
+
+        idx2 = load_list("idx2", offs2)
+        tab2_w = kept("tab2_w", [P, TC], I32)
+        nc.sync.dma_start(tab2_w[:], tab2_words[0].rearrange("p n i -> p (n i)").bitcast(I32))
+        w2_w = kept("w2_w", [P, 2 * H], U8)
+        nc.sync.dma_start(w2_w[:].bitcast(I32), w2_words[0].bitcast(I32))
+        for q in range(4):
+            nc.sync.dma_start(tab2_s[32 * q : 32 * q + 4, :].bitcast(I32), tab2_scales[0, 4 * q : 4 * q + 4, :].bitcast(I32))
+        for q in range(4):
+            nc.sync.dma_start(w2_s[32 * q : 32 * q + 4, :].bitcast(I32), w2_scales[0, 4 * q : 4 * q + 4, :].bitcast(I32))
+
+        def load_gate(tile, src, t0, t1):
+            rows = src.rearrange("(q t) j -> q t j", t=PACK)
+            for q in (0, 2, 1, 3):
+                nc.sync.dma_start(tile[32 * q : 32 * q + 32, t0:t1, :], rows[:, t0:t1, :])
+
+        page_rows = page0.rearrange("(b p t) c -> b t p c", b=2, t=PACK)
+        pages = [kept("page%d" % s, [P, T2], F32) for s in range(8)]
+
+        def load_page(s):
+            nc.sync.dma_start(pages[s][:], page_rows[s // PACK, s % PACK])
+
+        def load_weight(slot, src, row0, col0):
+            raw = in_slot(slot, "raw", [P, PACK, PASS], F32)
+            nc.sync.dma_start(raw[:], src[row0 : row0 + PASS, col0 : col0 + PASS].rearrange("(p i) c -> p i c", i=PACK))
+            return raw
+
+        def load_rows(name, src):
+            tile = kept(name, [P, 2, PACK], F32)
+            nc.sync.dma_start(tile[:], src.rearrange("(b p t) -> p b t", b=2, t=PACK))
+            return tile
+
+        gate2 = kept("gate2", [P, PACK, S], F32)
+        gate1 = kept("gate1", [P, PACK, S], F32)
+        load_page(0)
+        load_gate(gate2, wg2, 0, 1)
+        idx4 = load_list("idx4", offs4)
+        w4_raw = in_slot("even", "w4_raw", [P, 2, 2 * N], U8)
+        nc.sync.dma_start(w4_raw[:].bitcast(I32), w4_words.bitcast(I32).rearrange("b p n -> p b n"))
+        w5_raw = in_slot("odd", "w5_raw", [P, 2, N], I32)
+        nc.sync.dma_start(w5_raw[:], w5_words.rearrange("b p n i -> b p (n i)").bitcast(I32).rearrange("b p n -> p b n"))
+        load_gate(gate2, wg2, 1, PACK)
+        load_page(1)
+        load_page(2)
+        idx = load_list("idx", offs)
+        load_page(3)
+        for q in range(4):
+            nc.sync.dma_start(tab_s[32 * q : 32 * q + 8, :].bitcast(I32), tab_scales[:, 4 * q : 4 * q + 4, :].bitcast(I32))
+        tab_w = [in_slot("wide%d" % a, "tab_w%d" % a, [P, T], I32) for a in range(2)]
+        for a in range(2):
+            nc.sync.dma_start(tab_w[a][:], tab_words[a].rearrange("p n i -> p (n i)").bitcast(I32))
+        g1_rows = load_rows("g1_rows", g1)
+        load_page(4)
+        w1_raw = {}
+        for a in range(2):
+            w1_raw[a, 0] = load_weight("wide%d" % (2 + a), w1, PASS * a, 0)
+        load_page(5)
+        load_gate(gate1, wg1, 0, PACK)
+        idx3 = load_list("idx3", offs3)
+        load_page(6)
+        idx5 = load_list("idx5", offs5)
+        rg_rows = load_rows("rg_rows", rg)
+        load_page(7)
+        for first_row, src in ((0, w4_scales), (4, w5_scales)):
+            for q in range(4):
+                nc.sync.dma_start(
+                    w45_s_raw[32 * q + first_row : 32 * q + first_row + 4, :].bitcast(I32).rearrange("r (b n) -> r b n", b=2),
+                    src[:, 4 * q : 4 * q + 4, :].bitcast(I32).rearrange("b r n -> r b n"),
+                )
+
+        v2_w = kept("v2_w", [P, S], U32)
+        v2_s = kept("v2_s", [P, S], U8)
+        nc.vector.tensor_copy(v2_w[:], tab2_w[:].bitcast(U32).indirect(idx2[:]))
+        nc.vector.tensor_copy(v2_s[:], tab2_s[:].indirect(idx2[:]))
+
+        w4_w = kept("w4_w", [P, 2, 2 * N], U8)
+        nc.vector.tensor_copy(
+            w4_w[:].rearrange("p b (t m e) -> p b m t e", t=PACK, e=2),
+            w4_raw[:].rearrange("p b (m t e) -> p b m t e", t=PACK, e=2),
+        )
+        w5_w = kept("w5_w", [P, 2, N], I32)
+        nc.vector.tensor_copy(
+            w5_w[:].rearrange("p b (t m) -> p b m t", t=PACK),
+            w5_raw[:].rearrange("p b (m t) -> p b m t", t=PACK),
+        )
+
+        h2 = {}
+        for b in range(2):
+            magnitude = in_slot("magnitude", "magnitude", [P, PACK, PACK, P], F32)
+            for jt in range(S // P):
+                cols = slice(P * jt, P * (jt + 1))
+                acc = bank_b("acc2")
+                nc.tensor.matmul_mx(
+                    acc[:], lhsT=v2_w[:, cols].bitcast(FP8X4), lhsT_scale=v2_s[:, cols],
+                    rhs=w2_w[:, 2 * PASS * b : 2 * PASS * (b + 1)].bitcast(FP4X4), rhs_scale=w2_s[:, PASS * b : PASS * (b + 1)],
+                    start=True, stop=True,
+                )
+                nc.scalar.activation(magnitude[:, jt], acc[:].rearrange("j (m t) -> j t m", t=PACK), ACT.Abs)
+            for t in range(PACK):
+                turned = bank_a("turned")
+                for jt in range(S // P):
+                    nc.tensor.transpose(turned[:, P * jt : P * (jt + 1)], magnitude[:, jt, t, :], ident[:])
+                h2[b, t] = f512("h2")
+                nc.scalar.activation(h2[b, t][:], turned[:], ACT.Sqrt)
+
+        def scatter2(b, t):
+            nc.vector.tensor_tensor(pages[PACK * b + t][:].indirect(idx4[:]), h2[b, t][:], gate2[:, t, :], MULT)
+
+        for t in range(PACK):
+            scatter2(0, t)
+
+        v_w = [kept("v_w%d" % a, [P, S], U32) for a in range(2)]
+        v_s = kept("v_s", [P, S], U8)
+        for a in range(2):
+            nc.vector.tensor_copy(v_w[a][:], tab_w[a][:].bitcast(U32).indirect(idx[:]))
+        nc.vector.tensor_copy(v_s[:], tab_s[:].indirect(idx[:]))
+
+        w45_s = kept("w45_s", [P, 2 * N], U8)
+        nc.vector.tensor_copy(
+            w45_s[:].rearrange("p (b t m) -> p b m t", b=2, t=PACK),
+            w45_s_raw[:].rearrange("p (b m t) -> p b m t", b=2, t=PACK),
+        )
+
+        halves = ("even", "odd")
+
+        def quantise_weight(name, raw, slot):
+            rounded = in_slot(slot, "rounded", [P, PASS * PACK], BF16)
+            nc.scalar.copy(
+                rounded[:].rearrange("p (t m i) -> p m i t", t=PACK, i=PACK),
+                raw[:].rearrange("p i (m t) -> p m i t", t=PACK),
+            )
+            codes = kept(name + "_w", [P, PASS], U32)
+            plane = kept(name + "_s", [P, PASS], U8)
+            nc.vector.quantize_mx(codes[:].bitcast(FP8X4), plane[:], rounded[:])
+            return codes, plane
+
+        w1_q = {}
+        for a in range(2):
+            w1_q[a, 0] = quantise_weight("w1_%d0" % a, w1_raw[a, 0], halves[a])
+        for t in range(PACK):
+            scatter2(1, t)
+
+        def stream1(b, t):
+            cols = slice(P * t, P * (t + 1))
+            acc = bank_a("acc1")
+            for a in range(2):
+                codes, plane = w1_q[a, b]
+                nc.tensor.matmul_mx(
+                    acc[:], lhsT=codes[:, cols].bitcast(FP8X4), lhsT_scale=plane[:, cols],
+                    rhs=v_w[a][:].bitcast(FP8X4), rhs_scale=v_s[4 * a : P, :],
+                    start=(a == 0), stop=(a == 1),
+                )
+            squashed = f512("squashed")
+            nc.scalar.activation(squashed[:], acc[:], ACT.Tanh)
+            h1 = in_slot(halves[t % 2], "h1", [P, S], F32) if (b == 1 and t >= 2) else f512("h1")
+            nc.scalar.activation(h1[:], squashed[:], ACT.Copy, scale=g1_rows[:, b, t : t + 1])
+            nc.vector.tensor_tensor(pages[PACK * b + t][:].indirect(idx3[:]), h1[:], gate1[:, t, :], MULT)
+
+        for t in range(PACK):
+            stream1(0, t)
+        for a in range(2):
+            w1_q[a, 1] = quantise_weight("w1_%d1" % a, load_weight("wide%d" % a, w1, PASS * a, PASS), halves[a])
+        w3_raw = [load_weight("wide%d" % (2 + b), w3, PASS * b, 0) for b in range(2)]
+        for t in range(2):
+            stream1(1, t)
+        w3_q = [quantise_weight("w3_%d" % b, w3_raw[b], "spare%d" % b) for b in range(2)]
+
+        x_w = [kept("x_w%d" % b, [P, PICK], U32) for b in range(2)]
+        x_s = [kept("x_s%d" % b, [P, PICK], U8) for b in range(2)]
+
+        def weave(out, planes):
+            nc.scalar.copy(
+                out.rearrange("p (c i t) -> p c t i", i=PACK, t=PACK),
+                planes.rearrange("p t (c i) -> p c t i", i=PACK),
+            )
+
+        x_planes = in_slot("wide3", "x_planes", [P, PACK, PICK], BF16)
+        for t in range(PACK):
+            picked = in_slot(halves[t % 2], "picked", [P, PICK], F32)
+            nc.vector.tensor_copy(picked[:], pages[t][:].indirect(idx5[:]))
+            nc.scalar.activation(x_planes[:, t, :], picked[:], ACT.Copy, scale=rg_rows[:, 0, t : t + 1])
+        for t in range(2, PACK):
+            stream1(1, t)
+        for half in range(2):
+            cols = slice(PASS * half, PASS * (half + 1))
+            woven = in_slot("spare%d" % half, "woven", [P, PASS * PACK], BF16)
+            weave(woven[:], x_planes[:, :, cols])
+            nc.vector.quantize_mx(x_w[0][:, cols].bitcast(FP8X4), x_s[0][:, cols], woven[:])
+
+        y_w = kept("y_w", [P, PICK], U32)
+        y_s = kept("y_s", [P, PICK], U8)
+        y_rows = out_0.rearrange("(p t) j -> p t j", t=PACK)
+        y_words = out_1[0].rearrange("p m i -> p (m i)").bitcast(I32)
+
+        def pick_chunk(c):
+            picked = in_slot(halves[c % 2], "picked_chunk", [P, PACK, CHUNK], F32)
+            planes = ring.tile([P, PACK, CHUNK], BF16, name="planes_chunk", align_bytes=64)
+            offsets = idx5[:, CHUNK // 16 * c : CHUNK // 16 * (c + 1)]
+            for t in range(PACK):
+                nc.vector.tensor_copy(picked[:, t, :], pages[PACK + t][:].indirect(offsets))
+                nc.scalar.activation(planes[:, t, :], picked[:, t, :], ACT.Copy, scale=rg_rows[:, 1, t : t + 1])
+            for half in range(CHUNK // P):
+                cols = slice(CHUNK * c + P * half, CHUNK * c + P * (half + 1))
+                woven = ring.tile([P, PASS], BF16, name="woven_tile", align_bytes=64)
+                weave(woven[:], planes[:, :, P * half : P * (half + 1)])
+                nc.vector.quantize_mx(x_w[1][:, cols].bitcast(FP8X4), x_s[1][:, cols], woven[:])
+
+        def stationary(which, b, t):
+            cols = slice(P * t, P * (t + 1))
+            plane_cols = slice(N * b + P * t, N * b + P * (t + 1))
+            if which == 3:
+                codes, plane = w3_q[b]
+                return codes[:, cols].bitcast(FP8X4), plane[:, cols]
+            if which == 4:
+                return w4_w[:, b, 2 * P * t : 2 * P * (t + 1)].bitcast(FP4X4), w45_s[:, plane_cols]
+            return w5_w[:, b, cols].bitcast(FP8X4), w45_s[4:P, plane_cols]
+
+        def features(jt, y3):
+            cols = slice(P * jt, P * (jt + 1))
+            acc = {which: bank_b("acc%d" % which) for which in (3, 4, 5)}
+            for b in range(2):
+                for which in (3, 4, 5):
+                    for t in range(PACK):
+                        codes, plane = stationary(which, b, t)
+                        nc.tensor.matmul_mx(
+                            acc[which][:, P * t : P * (t + 1)], lhsT=codes, lhsT_scale=plane,
+                            rhs=x_w[b][:, cols].bitcast(FP8X4), rhs_scale=x_s[b][:, cols],
+                            start=(b == 0 and t == 0), stop=(b == 1 and t == PACK - 1),
+                        )
+            nc.scalar.copy(y3, acc[3][:])
+            product = f512("product")
+            nc.vector.tensor_tensor(product[:], acc[4][:], y3, MULT)
+            y = f512("y")
+            nc.vector.tensor_tensor(y[:], acc[5][:], product[:], ADD)
+            y_planes = y[:].rearrange("p (t j) -> p t j", t=PACK)
+            nc.sync.dma_start(y_rows[:, :, cols], y_planes)
+            rounded = ring.tile([P, PASS], BF16, name="y_rounded", align_bytes=64)
+            weave(rounded[:], y_planes)
+            nc.vector.quantize_mx(y_w[:, cols].bitcast(FP8X4), y_s[:, cols], rounded[:])
+
+        pick_chunk(0)
+        pick_chunk(1)
+        for c in range(PICK // CHUNK):
+            y3 = in_slot(halves[c % 2], "y3", [P, CHUNK // P, S], F32)
+            for half in range(CHUNK // P):
+                features(CHUNK // P * c + half, y3[:, half, :])
+            if c + 2 < PICK // CHUNK:
+                pick_chunk(c + 2)
+            cols = slice(CHUNK * c, CHUNK * (c + 1))
+            nc.sync.dma_start(y_words[:, cols], y_w[:, cols].bitcast(I32))
+        for q in range(4):
+            queue = nc.sync if q % 2 == 0 else nc.scalar
+            queue.dma_start(out_2[0, 4 * q : 4 * q + 4, :].bitcast(I32), y_s[32 * q : 32 * q + 4, :].bitcast(I32))

@@ -22,6 +22,16 @@ P = 128
 PACK = 4
 PASS = P * PACK
 CHUNK = 256
+EARLY=768
+LATE_SLOT={3:"even"}
+Y3_SLOT={1:"even"}
+AFTER={1:3}
+FIRST=3
+TAG_A="bank_a"
+BUF_A=2
+BUF_B=6
+WARM=True
+GAIN_SLOT={(1,3):"spare1"}
 
 
 def tile_list_electrolyser_slot_features_kernel(
@@ -56,33 +66,26 @@ def tile_list_electrolyser_slot_features_kernel(
             return ring.tile([P, S], F32, name=name, tag="f512", bufs=12, align_bytes=64)
 
         def bank_a(name):
-            return psum.tile([P, S], F32, name=name, tag="bank_a", bufs=2)
+            return psum.tile([P, S], F32, name=name, tag=TAG_A, bufs=BUF_A)
 
         def bank_b(name):
-            return psum.tile([P, S], F32, name=name, tag="bank_b", bufs=6)
+            return psum.tile([P, S], F32, name=name, tag="bank_b", bufs=BUF_B)
 
         tab2_s = zeroed_plane("tab2_s", TC, nc.gpsimd)
         w2_s = zeroed_plane("w2_s", H, nc.gpsimd)
-        tab_s = zeroed_plane("tab_s", T, nc.vector)
-        w45_s_raw = zeroed_plane("w45_s_raw", 2 * N, nc.vector)
-
+        if WARM:
+            warm = kept("warm", [P, 2], F32)
+            nc.gpsimd.memset(warm[:], 1.0)
+            nc.scalar.activation(warm[:, 1:2], warm[:, 0:1], ACT.Sqrt)
         ident = kept("ident", [P, P], F32)
         make_identity(nc, ident[:])
+        tab_s = zeroed_plane("tab_s", T, nc.gpsimd)
+        w45_s_raw = zeroed_plane("w45_s_raw", 2 * N, nc.gpsimd)
 
-        idx2 = load_list("idx2", offs2)
-        tab2_w = kept("tab2_w", [P, TC], I32)
-        nc.sync.dma_start(tab2_w[:], tab2_words[0].rearrange("p n i -> p (n i)").bitcast(I32))
-        w2_w = kept("w2_w", [P, 2 * H], U8)
-        nc.sync.dma_start(w2_w[:].bitcast(I32), w2_words[0].bitcast(I32))
-        for q in range(4):
-            nc.sync.dma_start(tab2_s[32 * q : 32 * q + 4, :].bitcast(I32), tab2_scales[0, 4 * q : 4 * q + 4, :].bitcast(I32))
-        for q in range(4):
-            nc.sync.dma_start(w2_s[32 * q : 32 * q + 4, :].bitcast(I32), w2_scales[0, 4 * q : 4 * q + 4, :].bitcast(I32))
-
-        def load_gate(tile, src, t0, t1):
-            rows = src.rearrange("(q t) j -> q t j", t=PACK)
-            for q in (0, 2, 1, 3):
-                nc.sync.dma_start(tile[32 * q : 32 * q + 32, t0:t1, :], rows[:, t0:t1, :])
+        def load_gate(name, src):
+            tile = in_slot("gate_rows", name, [P, S], F32)
+            nc.sync.dma_start(tile[:], src)
+            return tile
 
         page_rows = page0.rearrange("(b p t) c -> b t p c", b=2, t=PACK)
         pages = [kept("page%d" % s, [P, T2], F32) for s in range(8)]
@@ -100,43 +103,70 @@ def tile_list_electrolyser_slot_features_kernel(
             nc.sync.dma_start(tile[:], src.rearrange("(b p t) -> p b t", b=2, t=PACK))
             return tile
 
-        gate2 = kept("gate2", [P, PACK, S], F32)
-        gate1 = kept("gate1", [P, PACK, S], F32)
-        load_page(0)
-        load_gate(gate2, wg2, 0, 1)
-        idx4 = load_list("idx4", offs4)
+        def load_plane(plane, first_row, rows, src):
+            for q in range(4):
+                nc.sync.dma_start(plane[32 * q + first_row : 32 * q + first_row + rows, :].bitcast(I32), src[:, 4 * q : 4 * q + 4, :].bitcast(I32))
+
+        idx2 = load_list("idx2", offs2)
+        tab2_w = kept("tab2_w", [P, TC], I32)
+        nc.sync.dma_start(tab2_w[:], tab2_words[0].rearrange("p n i -> p (n i)").bitcast(I32))
+        wg2_rows = load_gate("wg2_rows", wg2)
+        load_plane(tab2_s, 0, 4, tab2_scales)
+        w2_w = kept("w2_w", [P, 2 * H], U8)
+        nc.sync.dma_start(w2_w[:].bitcast(I32), w2_words[0].bitcast(I32))
+        load_plane(w2_s, 0, 4, w2_scales)
         w4_raw = in_slot("even", "w4_raw", [P, 2, 2 * N], U8)
         nc.sync.dma_start(w4_raw[:].bitcast(I32), w4_words.bitcast(I32).rearrange("b p n -> p b n"))
         w5_raw = in_slot("odd", "w5_raw", [P, 2, N], I32)
         nc.sync.dma_start(w5_raw[:], w5_words.rearrange("b p n i -> b p (n i)").bitcast(I32).rearrange("b p n -> p b n"))
-        load_gate(gate2, wg2, 1, PACK)
+        load_page(0)
+        idx4 = load_list("idx4", offs4)
         load_page(1)
         load_page(2)
         idx = load_list("idx", offs)
         load_page(3)
-        for q in range(4):
-            nc.sync.dma_start(tab_s[32 * q : 32 * q + 8, :].bitcast(I32), tab_scales[:, 4 * q : 4 * q + 4, :].bitcast(I32))
+        load_plane(tab_s, 0, 8, tab_scales)
         tab_w = [in_slot("wide%d" % a, "tab_w%d" % a, [P, T], I32) for a in range(2)]
         for a in range(2):
             nc.sync.dma_start(tab_w[a][:], tab_words[a].rearrange("p n i -> p (n i)").bitcast(I32))
-        g1_rows = load_rows("g1_rows", g1)
-        load_page(4)
         w1_raw = {}
-        for a in range(2):
-            w1_raw[a, 0] = load_weight("wide%d" % (2 + a), w1, PASS * a, 0)
+        load_page(4)
+        w1_raw[0, 0] = load_weight("wide2", w1, PASS * 0, 0)
         load_page(5)
-        load_gate(gate1, wg1, 0, PACK)
-        idx3 = load_list("idx3", offs3)
+        w1_raw[1, 0] = load_weight("wide3", w1, PASS * 1, 0)
         load_page(6)
+        wg1_rows = load_gate("wg1_rows", wg1)
+        g1_rows = load_rows("g1_rows", g1)
+        idx3 = load_list("idx3", offs3)
         idx5 = load_list("idx5", offs5)
         rg_rows = load_rows("rg_rows", rg)
         load_page(7)
-        for first_row, src in ((0, w4_scales), (4, w5_scales)):
-            for q in range(4):
-                nc.sync.dma_start(
-                    w45_s_raw[32 * q + first_row : 32 * q + first_row + 4, :].bitcast(I32).rearrange("r (b n) -> r b n", b=2),
-                    src[:, 4 * q : 4 * q + 4, :].bitcast(I32).rearrange("b r n -> r b n"),
+        def dealt(acc):
+            return acc[:].rearrange("j (m t) -> j t m", t=PACK)
+
+        def turn_gate(rows, turned_gate):
+            for jt in range(S // P):
+                acc = bank_b("gate_t")
+                nc.tensor.transpose(acc[:, 0:P], rows[:, P * jt : P * (jt + 1)], ident[:])
+                by_t = acc[:, 0:P].rearrange("j (q t) -> j t q", t=PACK)
+                nc.scalar.copy(
+                    turned_gate[:, jt].rearrange("j t (copy q) -> j t copy q", copy=4),
+                    by_t.unsqueeze(2).broadcast_to([P, PACK, 4, 32]),
                 )
+
+        def turn_back(acc, turned, t):
+            for jt in range(S // P):
+                nc.tensor.transpose(acc[:, P * jt : P * (jt + 1)], turned[:, jt, t, :], ident[:])
+
+        gate2_t = in_slot("gate_t", "gate2_t", [P, PACK, PACK, P], F32)
+        turn_gate(wg2_rows, gate2_t)
+        gate2 = kept("gate2", [P, PACK, S], F32)
+
+        def make_gate2(t):
+            acc = bank_b("gate2_acc")
+            turn_back(acc, gate2_t, t)
+            nc.vector.tensor_copy(gate2[:, t, :], acc[:])
+
 
         v2_w = kept("v2_w", [P, S], U32)
         v2_s = kept("v2_s", [P, S], U8)
@@ -145,8 +175,8 @@ def tile_list_electrolyser_slot_features_kernel(
 
         w4_w = kept("w4_w", [P, 2, 2 * N], U8)
         nc.vector.tensor_copy(
-            w4_w[:].rearrange("p b (t m e) -> p b m t e", t=PACK, e=2),
-            w4_raw[:].rearrange("p b (m t e) -> p b m t e", t=PACK, e=2),
+            w4_w[:].rearrange("p b (t m e) -> p b t m e", t=PACK, e=2),
+            w4_raw[:].rearrange("p b (m t e) -> p b t m e", t=PACK, e=2),
         )
         w5_w = kept("w5_w", [P, 2, N], I32)
         nc.vector.tensor_copy(
@@ -165,11 +195,12 @@ def tile_list_electrolyser_slot_features_kernel(
                     rhs=w2_w[:, 2 * PASS * b : 2 * PASS * (b + 1)].bitcast(FP4X4), rhs_scale=w2_s[:, PASS * b : PASS * (b + 1)],
                     start=True, stop=True,
                 )
-                nc.scalar.activation(magnitude[:, jt], acc[:].rearrange("j (m t) -> j t m", t=PACK), ACT.Abs)
+                nc.scalar.activation(magnitude[:, jt], dealt(acc), ACT.Abs)
             for t in range(PACK):
+                if b == 0:
+                    make_gate2(t)
                 turned = bank_a("turned")
-                for jt in range(S // P):
-                    nc.tensor.transpose(turned[:, P * jt : P * (jt + 1)], magnitude[:, jt, t, :], ident[:])
+                turn_back(turned, magnitude, t)
                 h2[b, t] = f512("h2")
                 nc.scalar.activation(h2[b, t][:], turned[:], ACT.Sqrt)
 
@@ -184,12 +215,6 @@ def tile_list_electrolyser_slot_features_kernel(
         for a in range(2):
             nc.vector.tensor_copy(v_w[a][:], tab_w[a][:].bitcast(U32).indirect(idx[:]))
         nc.vector.tensor_copy(v_s[:], tab_s[:].indirect(idx[:]))
-
-        w45_s = kept("w45_s", [P, 2 * N], U8)
-        nc.vector.tensor_copy(
-            w45_s[:].rearrange("p (b t m) -> p b m t", b=2, t=PACK),
-            w45_s_raw[:].rearrange("p (b m t) -> p b m t", b=2, t=PACK),
-        )
 
         halves = ("even", "odd")
 
@@ -210,6 +235,9 @@ def tile_list_electrolyser_slot_features_kernel(
         for t in range(PACK):
             scatter2(1, t)
 
+        gate1_t = in_slot("gate_t", "gate1_t", [P, PACK, PACK, P], F32)
+        turn_gate(wg1_rows, gate1_t)
+
         def stream1(b, t):
             cols = slice(P * t, P * (t + 1))
             acc = bank_a("acc1")
@@ -222,18 +250,11 @@ def tile_list_electrolyser_slot_features_kernel(
                 )
             squashed = f512("squashed")
             nc.scalar.activation(squashed[:], acc[:], ACT.Tanh)
-            h1 = in_slot(halves[t % 2], "h1", [P, S], F32) if (b == 1 and t >= 2) else f512("h1")
-            nc.scalar.activation(h1[:], squashed[:], ACT.Copy, scale=g1_rows[:, b, t : t + 1])
-            nc.vector.tensor_tensor(pages[PACK * b + t][:].indirect(idx3[:]), h1[:], gate1[:, t, :], MULT)
-
-        for t in range(PACK):
-            stream1(0, t)
-        for a in range(2):
-            w1_q[a, 1] = quantise_weight("w1_%d1" % a, load_weight("wide%d" % a, w1, PASS * a, PASS), halves[a])
-        w3_raw = [load_weight("wide%d" % (2 + b), w3, PASS * b, 0) for b in range(2)]
-        for t in range(2):
-            stream1(1, t)
-        w3_q = [quantise_weight("w3_%d" % b, w3_raw[b], "spare%d" % b) for b in range(2)]
+            gate_acc = bank_a("gate1_acc")
+            turn_back(gate_acc, gate1_t, t)
+            gain = in_slot(GAIN_SLOT[b, t], "gain", [P, S], F32) if (b, t) in GAIN_SLOT else f512("gain")
+            nc.scalar.activation(gain[:], gate_acc[:], ACT.Copy, scale=g1_rows[:, b, t : t + 1])
+            nc.vector.tensor_tensor(pages[PACK * b + t][:].indirect(idx3[:]), squashed[:], gain[:], MULT)
 
         x_w = [kept("x_w%d" % b, [P, PICK], U32) for b in range(2)]
         x_s = [kept("x_s%d" % b, [P, PICK], U8) for b in range(2)]
@@ -244,18 +265,56 @@ def tile_list_electrolyser_slot_features_kernel(
                 planes.rearrange("p t (c i) -> p c t i", i=PACK),
             )
 
-        x_planes = in_slot("wide3", "x_planes", [P, PACK, PICK], BF16)
-        for t in range(PACK):
-            picked = in_slot(halves[t % 2], "picked", [P, PICK], F32)
-            nc.vector.tensor_copy(picked[:], pages[t][:].indirect(idx5[:]))
-            nc.scalar.activation(x_planes[:, t, :], picked[:], ACT.Copy, scale=rg_rows[:, 0, t : t + 1])
-        for t in range(2, PACK):
-            stream1(1, t)
+        def pick(b, t, planes, width):
+            picked = in_slot(halves[t % 2], "picked", [P, width], F32)
+            nc.vector.tensor_copy(picked[:], pages[PACK * b + t][:].indirect(idx5[:, 0 : width // 16]))
+            nc.scalar.activation(planes[:, t, 0:width], picked[:], ACT.Copy, scale=rg_rows[:, b, t : t + 1])
+
+        for a in range(2):
+            w1_raw[a, 1] = load_weight("wide%d" % a, w1, PASS * a, PASS)
+        w3_raw = [load_weight("wide%d" % (2 + b), w3, PASS * b, 0) for b in range(2)]
+        for first_row, src in ((0, w4_scales), (4, w5_scales)):
+            for q in range(4):
+                nc.sync.dma_start(
+                    w45_s_raw[32 * q + first_row : 32 * q + first_row + 4, :].bitcast(I32).rearrange("r (b n) -> r b n", b=2),
+                    src[:, 4 * q : 4 * q + 4, :].bitcast(I32).rearrange("b r n -> r b n"),
+                )
+
+        planes0 = in_slot("magnitude", "planes0", [P, PACK, PICK], BF16)
+        stream1(0, 0)
+        stream1(0, 1)
+        for a in range(2):
+            w1_q[a, 1] = quantise_weight("w1_%d1" % a, w1_raw[a, 1], halves[a])
+        stream1(0, 2)
+        stream1(0, 3)
+        stream1(1, 0)
+        pick(0, 0, planes0, PICK)
+        pick(0, 1, planes0, PICK)
+        pick(0, 2, planes0, PICK)
+        pick(0, 3, planes0, PICK)
+        stream1(1, 1)
+        w3_q = [quantise_weight("w3_%d" % b, w3_raw[b], "spare%d" % b) for b in range(2)]
+        w45_s = kept("w45_s", [P, 2 * N], U8)
+        nc.vector.tensor_copy(
+            w45_s[:].rearrange("p (b t m) -> p b t m", b=2, t=PACK),
+            w45_s_raw[:].rearrange("p (b m t) -> p b t m", b=2, t=PACK),
+        )
+
         for half in range(2):
             cols = slice(PASS * half, PASS * (half + 1))
             woven = in_slot("spare%d" % half, "woven", [P, PASS * PACK], BF16)
-            weave(woven[:], x_planes[:, :, cols])
+            weave(woven[:], planes0[:, :, cols])
             nc.vector.quantize_mx(x_w[0][:, cols].bitcast(FP8X4), x_s[0][:, cols], woven[:])
+        stream1(1, 2)
+        stream1(1, 3)
+        planes1 = in_slot("wide0", "planes1", [P, PACK - 1, PICK], BF16)
+        pick(1, 0, planes1, EARLY)
+        pick(1, 1, planes1, EARLY)
+        pick(1, 2, planes1, EARLY)
+        woven1 = in_slot("wide1", "woven1", [P, PICK, PACK], BF16)
+        for half in range(2):
+            cols = slice(EARLY // 2 * half, EARLY // 2 * (half + 1))
+            nc.scalar.copy(woven1[:, cols, 0 : PACK - 1], planes1[:, :, cols].rearrange("p t c -> p c t"))
 
         y_w = kept("y_w", [P, PICK], U32)
         y_s = kept("y_s", [P, PICK], U8)
@@ -263,17 +322,20 @@ def tile_list_electrolyser_slot_features_kernel(
         y_words = out_1[0].rearrange("p m i -> p (m i)").bitcast(I32)
 
         def pick_chunk(c):
-            picked = in_slot(halves[c % 2], "picked_chunk", [P, PACK, CHUNK], F32)
-            planes = ring.tile([P, PACK, CHUNK], BF16, name="planes_chunk", align_bytes=64)
+            cols = slice(CHUNK * c, CHUNK * (c + 1))
             offsets = idx5[:, CHUNK // 16 * c : CHUNK // 16 * (c + 1)]
-            for t in range(PACK):
-                nc.vector.tensor_copy(picked[:, t, :], pages[PACK + t][:].indirect(offsets))
-                nc.scalar.activation(planes[:, t, :], picked[:, t, :], ACT.Copy, scale=rg_rows[:, 1, t : t + 1])
-            for half in range(CHUNK // P):
-                cols = slice(CHUNK * c + P * half, CHUNK * c + P * (half + 1))
-                woven = ring.tile([P, PASS], BF16, name="woven_tile", align_bytes=64)
-                weave(woven[:], planes[:, :, P * half : P * (half + 1)])
-                nc.vector.quantize_mx(x_w[1][:, cols].bitcast(FP8X4), x_s[1][:, cols], woven[:])
+            if CHUNK * c < EARLY:
+                late = [PACK - 1]
+                picked = ring.tile([P, 1, CHUNK], F32, name="picked_chunk", align_bytes=64, bufs=4)
+            else:
+                late = list(range(PACK))
+                picked = in_slot(LATE_SLOT[c], "picked_late", [P, PACK, CHUNK], F32)
+            for n, t in enumerate(late):
+                nc.vector.tensor_copy(picked[:, n, :], pages[PACK + t][:].indirect(offsets))
+                nc.scalar.activation(woven1[:, cols, t], picked[:, n, :], ACT.Copy, scale=rg_rows[:, 1, t : t + 1])
+            nc.vector.quantize_mx(
+                x_w[1][:, cols].bitcast(FP8X4), x_s[1][:, cols], woven1[:, cols, :].rearrange("p c t -> p (c t)")
+            )
 
         def stationary(which, b, t):
             cols = slice(P * t, P * (t + 1))
@@ -285,7 +347,7 @@ def tile_list_electrolyser_slot_features_kernel(
                 return w4_w[:, b, 2 * P * t : 2 * P * (t + 1)].bitcast(FP4X4), w45_s[:, plane_cols]
             return w5_w[:, b, cols].bitcast(FP8X4), w45_s[4:P, plane_cols]
 
-        def features(jt, y3):
+        def features(jt):
             cols = slice(P * jt, P * (jt + 1))
             acc = {which: bank_b("acc%d" % which) for which in (3, 4, 5)}
             for b in range(2):
@@ -297,9 +359,10 @@ def tile_list_electrolyser_slot_features_kernel(
                             rhs=x_w[b][:, cols].bitcast(FP8X4), rhs_scale=x_s[b][:, cols],
                             start=(b == 0 and t == 0), stop=(b == 1 and t == PACK - 1),
                         )
-            nc.scalar.copy(y3, acc[3][:])
+            y3 = in_slot(Y3_SLOT[jt], "y3", [P, S], F32) if jt in Y3_SLOT else f512("y3")
+            nc.scalar.copy(y3[:], acc[3][:])
             product = f512("product")
-            nc.vector.tensor_tensor(product[:], acc[4][:], y3, MULT)
+            nc.vector.tensor_tensor(product[:], acc[4][:], y3[:], MULT)
             y = f512("y")
             nc.vector.tensor_tensor(y[:], acc[5][:], product[:], ADD)
             y_planes = y[:].rearrange("p (t j) -> p t j", t=PACK)
@@ -308,16 +371,15 @@ def tile_list_electrolyser_slot_features_kernel(
             weave(rounded[:], y_planes)
             nc.vector.quantize_mx(y_w[:, cols].bitcast(FP8X4), y_s[:, cols], rounded[:])
 
-        pick_chunk(0)
-        pick_chunk(1)
-        for c in range(PICK // CHUNK):
-            y3 = in_slot(halves[c % 2], "y3", [P, CHUNK // P, S], F32)
-            for half in range(CHUNK // P):
-                features(CHUNK // P * c + half, y3[:, half, :])
-            if c + 2 < PICK // CHUNK:
-                pick_chunk(c + 2)
-            cols = slice(CHUNK * c, CHUNK * (c + 1))
-            nc.sync.dma_start(y_words[:, cols], y_w[:, cols].bitcast(I32))
+        for c in range(FIRST):
+            pick_chunk(c)
+        for jt in range(PICK // P):
+            features(jt)
+            if jt in AFTER:
+                pick_chunk(AFTER[jt])
+            if jt % 2 == 1:
+                cols = slice(P * (jt - 1), P * (jt + 1))
+                nc.sync.dma_start(y_words[:, cols], y_w[:, cols].bitcast(I32))
         for q in range(4):
             queue = nc.sync if q % 2 == 0 else nc.scalar
             queue.dma_start(out_2[0, 4 * q : 4 * q + 4, :].bitcast(I32), y_s[32 * q : 32 * q + 4, :].bitcast(I32))

@@ -21,17 +21,12 @@ FLOPS = 2 * (K * H * S + K2 * H * S + 3 * H * N * PICK)
 P = 128
 PACK = 4
 PASS = P * PACK
+QUADS = 4
+LIST_ROWS = 16
 CHUNK = 256
-EARLY=768
-LATE_SLOT={3:"even"}
-Y3_SLOT={1:"even"}
-AFTER={1:3}
-FIRST=3
-TAG_A="bank_a"
-BUF_A=2
-BUF_B=6
-WARM=True
-GAIN_SLOT={(1,3):"spare1"}
+EARLY = PICK - CHUNK
+GATES_ON_VECTOR = 2
+WORK_TILES = 12
 
 
 def tile_list_electrolyser_slot_features_kernel(
@@ -49,124 +44,120 @@ def tile_list_electrolyser_slot_features_kernel(
         def kept(name, shape, dtype):
             return keep.tile(shape, dtype, name=name, align_bytes=64)
 
+        def in_slot(slot, name, shape, dtype):
+            return ring.tile(shape, dtype, name=name, tag=slot, bufs=1, align_bytes=64)
+
+        def work_tile(name):
+            return ring.tile([P, S], F32, name=name, tag="work", bufs=WORK_TILES, align_bytes=64)
+
+        def short_bank(name):
+            return psum.tile([P, S], F32, name=name, tag="short_bank", bufs=2)
+
+        def long_bank(name):
+            return psum.tile([P, S], F32, name=name, tag="long_bank", bufs=6)
+
+        def zeroed_plane(name, width):
+            plane = kept(name, [P, width], U8)
+            nc.gpsimd.memset(plane[:].bitcast(I32), 0)
+            return plane
+
+        tab2_s = zeroed_plane("tab2_s", TC)
+        w2_s = zeroed_plane("w2_s", H)
+        ident = kept("ident", [P, P], F32)
+        make_identity(nc, ident[:])
+        tab_s = zeroed_plane("tab_s", T)
+        w45_s_raw = zeroed_plane("w45_s_raw", 2 * N)
+
+        page_rows = page0.rearrange("(b p t) c -> b t p c", b=2, t=PACK)
+        pages = {(b, t): kept("page%d%d" % (b, t), [P, T2], F32) for b in range(2) for t in range(PACK)}
+
         def load_list(name, src):
             tile = lists.tile(list(src.shape), U16, name=name)
             nc.sync.dma_start(tile[:], src)
             return tile
 
-        def zeroed_plane(name, width, engine):
-            plane = kept(name, [P, width], U8)
-            engine.memset(plane[:].bitcast(I32), 0)
-            return plane
-
-        def in_slot(slot, name, shape, dtype):
-            return ring.tile(shape, dtype, name=name, tag=slot, bufs=1, align_bytes=64)
-
-        def f512(name):
-            return ring.tile([P, S], F32, name=name, tag="f512", bufs=12, align_bytes=64)
-
-        def bank_a(name):
-            return psum.tile([P, S], F32, name=name, tag=TAG_A, bufs=BUF_A)
-
-        def bank_b(name):
-            return psum.tile([P, S], F32, name=name, tag="bank_b", bufs=BUF_B)
-
-        tab2_s = zeroed_plane("tab2_s", TC, nc.gpsimd)
-        w2_s = zeroed_plane("w2_s", H, nc.gpsimd)
-        if WARM:
-            warm = kept("warm", [P, 2], F32)
-            nc.gpsimd.memset(warm[:], 1.0)
-            nc.scalar.activation(warm[:, 1:2], warm[:, 0:1], ACT.Sqrt)
-        ident = kept("ident", [P, P], F32)
-        make_identity(nc, ident[:])
-        tab_s = zeroed_plane("tab_s", T, nc.gpsimd)
-        w45_s_raw = zeroed_plane("w45_s_raw", 2 * N, nc.gpsimd)
+        def load_page(b, t):
+            nc.sync.dma_start(pages[b, t][:], page_rows[b, t])
 
         def load_gate(name, src):
             tile = in_slot("gate_rows", name, [P, S], F32)
             nc.sync.dma_start(tile[:], src)
             return tile
 
-        page_rows = page0.rearrange("(b p t) c -> b t p c", b=2, t=PACK)
-        pages = [kept("page%d" % s, [P, T2], F32) for s in range(8)]
-
-        def load_page(s):
-            nc.sync.dma_start(pages[s][:], page_rows[s // PACK, s % PACK])
-
         def load_weight(slot, src, row0, col0):
             raw = in_slot(slot, "raw", [P, PACK, PASS], F32)
             nc.sync.dma_start(raw[:], src[row0 : row0 + PASS, col0 : col0 + PASS].rearrange("(p i) c -> p i c", i=PACK))
             return raw
 
-        def load_rows(name, src):
+        def load_row_gains(name, src):
             tile = kept(name, [P, 2, PACK], F32)
             nc.sync.dma_start(tile[:], src.rearrange("(b p t) -> p b t", b=2, t=PACK))
             return tile
 
-        def load_plane(plane, first_row, rows, src):
-            for q in range(4):
-                nc.sync.dma_start(plane[32 * q + first_row : 32 * q + first_row + rows, :].bitcast(I32), src[:, 4 * q : 4 * q + 4, :].bitcast(I32))
+        def load_plane(plane, src):
+            rows = 4 * src.shape[0]
+            for quad in range(QUADS):
+                nc.sync.dma_start(plane[32 * quad : 32 * quad + rows, :].bitcast(I32), src[:, 4 * quad : 4 * quad + 4, :].bitcast(I32))
 
         idx2 = load_list("idx2", offs2)
         tab2_w = kept("tab2_w", [P, TC], I32)
         nc.sync.dma_start(tab2_w[:], tab2_words[0].rearrange("p n i -> p (n i)").bitcast(I32))
         wg2_rows = load_gate("wg2_rows", wg2)
-        load_plane(tab2_s, 0, 4, tab2_scales)
+        load_plane(tab2_s, tab2_scales)
         w2_w = kept("w2_w", [P, 2 * H], U8)
         nc.sync.dma_start(w2_w[:].bitcast(I32), w2_words[0].bitcast(I32))
-        load_plane(w2_s, 0, 4, w2_scales)
+        load_plane(w2_s, w2_scales)
         w4_raw = in_slot("even", "w4_raw", [P, 2, 2 * N], U8)
         nc.sync.dma_start(w4_raw[:].bitcast(I32), w4_words.bitcast(I32).rearrange("b p n -> p b n"))
         w5_raw = in_slot("odd", "w5_raw", [P, 2, N], I32)
         nc.sync.dma_start(w5_raw[:], w5_words.rearrange("b p n i -> b p (n i)").bitcast(I32).rearrange("b p n -> p b n"))
-        load_page(0)
+        load_page(0, 0)
         idx4 = load_list("idx4", offs4)
-        load_page(1)
-        load_page(2)
+        load_page(0, 1)
+        load_page(0, 2)
         idx = load_list("idx", offs)
-        load_page(3)
-        load_plane(tab_s, 0, 8, tab_scales)
+        load_page(0, 3)
+        load_plane(tab_s, tab_scales)
         tab_w = [in_slot("wide%d" % a, "tab_w%d" % a, [P, T], I32) for a in range(2)]
         for a in range(2):
             nc.sync.dma_start(tab_w[a][:], tab_words[a].rearrange("p n i -> p (n i)").bitcast(I32))
         w1_raw = {}
-        load_page(4)
-        w1_raw[0, 0] = load_weight("wide2", w1, PASS * 0, 0)
-        load_page(5)
-        w1_raw[1, 0] = load_weight("wide3", w1, PASS * 1, 0)
-        load_page(6)
+        for a in range(2):
+            load_page(1, a)
+            w1_raw[a, 0] = load_weight("wide%d" % (2 + a), w1, PASS * a, 0)
+        load_page(1, 2)
         wg1_rows = load_gate("wg1_rows", wg1)
-        g1_rows = load_rows("g1_rows", g1)
+        g1_rows = load_row_gains("g1_rows", g1)
         idx3 = load_list("idx3", offs3)
         idx5 = load_list("idx5", offs5)
-        rg_rows = load_rows("rg_rows", rg)
-        load_page(7)
-        def dealt(acc):
-            return acc[:].rearrange("j (m t) -> j t m", t=PACK)
+        rg_rows = load_row_gains("rg_rows", rg)
+        load_page(1, 3)
 
         def turn_gate(rows, turned_gate):
             for jt in range(S // P):
-                acc = bank_b("gate_t")
+                acc = long_bank("gate_turned")
                 nc.tensor.transpose(acc[:, 0:P], rows[:, P * jt : P * (jt + 1)], ident[:])
-                by_t = acc[:, 0:P].rearrange("j (q t) -> j t q", t=PACK)
+                by_t = acc[:, 0:P].rearrange("j (u t) -> j t u", t=PACK)
                 nc.scalar.copy(
-                    turned_gate[:, jt].rearrange("j t (copy q) -> j t copy q", copy=4),
-                    by_t.unsqueeze(2).broadcast_to([P, PACK, 4, 32]),
+                    turned_gate[:, jt].rearrange("j t (quad u) -> j t quad u", quad=QUADS),
+                    by_t.unsqueeze(2).broadcast_to([P, PACK, QUADS, P // QUADS]),
                 )
 
         def turn_back(acc, turned, t):
             for jt in range(S // P):
                 nc.tensor.transpose(acc[:, P * jt : P * (jt + 1)], turned[:, jt, t, :], ident[:])
 
-        gate2_t = in_slot("gate_t", "gate2_t", [P, PACK, PACK, P], F32)
-        turn_gate(wg2_rows, gate2_t)
+        gate2_turned = in_slot("gate_turned", "gate2_turned", [P, S // P, PACK, P], F32)
+        turn_gate(wg2_rows, gate2_turned)
         gate2 = kept("gate2", [P, PACK, S], F32)
 
         def make_gate2(t):
-            acc = bank_b("gate2_acc")
-            turn_back(acc, gate2_t, t)
-            nc.vector.tensor_copy(gate2[:, t, :], acc[:])
-
+            acc = long_bank("gate2_acc")
+            turn_back(acc, gate2_turned, t)
+            if t < GATES_ON_VECTOR:
+                nc.vector.tensor_copy(gate2[:, t, :], acc[:])
+            else:
+                nc.scalar.copy(gate2[:, t, :], acc[:])
 
         v2_w = kept("v2_w", [P, S], U32)
         v2_s = kept("v2_s", [P, S], U8)
@@ -186,29 +177,29 @@ def tile_list_electrolyser_slot_features_kernel(
 
         h2 = {}
         for b in range(2):
-            magnitude = in_slot("magnitude", "magnitude", [P, PACK, PACK, P], F32)
+            magnitude = in_slot("magnitude", "magnitude", [P, S // P, PACK, P], F32)
             for jt in range(S // P):
                 cols = slice(P * jt, P * (jt + 1))
-                acc = bank_b("acc2")
+                acc = long_bank("acc2")
                 nc.tensor.matmul_mx(
                     acc[:], lhsT=v2_w[:, cols].bitcast(FP8X4), lhsT_scale=v2_s[:, cols],
                     rhs=w2_w[:, 2 * PASS * b : 2 * PASS * (b + 1)].bitcast(FP4X4), rhs_scale=w2_s[:, PASS * b : PASS * (b + 1)],
                     start=True, stop=True,
                 )
-                nc.scalar.activation(magnitude[:, jt], dealt(acc), ACT.Abs)
+                nc.scalar.activation(magnitude[:, jt], acc[:].rearrange("j (m t) -> j t m", t=PACK), ACT.Abs)
             for t in range(PACK):
                 if b == 0:
                     make_gate2(t)
-                turned = bank_a("turned")
-                turn_back(turned, magnitude, t)
-                h2[b, t] = f512("h2")
-                nc.scalar.activation(h2[b, t][:], turned[:], ACT.Sqrt)
+                magnitude_acc = short_bank("magnitude_acc")
+                turn_back(magnitude_acc, magnitude, t)
+                h2[b, t] = work_tile("h2")
+                nc.scalar.activation(h2[b, t][:], magnitude_acc[:], ACT.Sqrt)
 
-        def scatter2(b, t):
-            nc.vector.tensor_tensor(pages[PACK * b + t][:].indirect(idx4[:]), h2[b, t][:], gate2[:, t, :], MULT)
+        def put_stream2(b, t):
+            nc.vector.tensor_tensor(pages[b, t][:].indirect(idx4[:]), h2[b, t][:], gate2[:, t, :], MULT)
 
         for t in range(PACK):
-            scatter2(0, t)
+            put_stream2(0, t)
 
         v_w = [kept("v_w%d" % a, [P, S], U32) for a in range(2)]
         v_s = kept("v_s", [P, S], U8)
@@ -216,7 +207,7 @@ def tile_list_electrolyser_slot_features_kernel(
             nc.vector.tensor_copy(v_w[a][:], tab_w[a][:].bitcast(U32).indirect(idx[:]))
         nc.vector.tensor_copy(v_s[:], tab_s[:].indirect(idx[:]))
 
-        halves = ("even", "odd")
+        parity_slots = ("even", "odd")
 
         def quantise_weight(name, raw, slot):
             rounded = in_slot(slot, "rounded", [P, PASS * PACK], BF16)
@@ -231,16 +222,16 @@ def tile_list_electrolyser_slot_features_kernel(
 
         w1_q = {}
         for a in range(2):
-            w1_q[a, 0] = quantise_weight("w1_%d0" % a, w1_raw[a, 0], halves[a])
+            w1_q[a, 0] = quantise_weight("w1_%d0" % a, w1_raw[a, 0], parity_slots[a])
         for t in range(PACK):
-            scatter2(1, t)
+            put_stream2(1, t)
 
-        gate1_t = in_slot("gate_t", "gate1_t", [P, PACK, PACK, P], F32)
-        turn_gate(wg1_rows, gate1_t)
+        gate1_turned = in_slot("gate_turned", "gate1_turned", [P, S // P, PACK, P], F32)
+        turn_gate(wg1_rows, gate1_turned)
 
-        def stream1(b, t):
+        def put_stream1(b, t, gain_slot=None):
             cols = slice(P * t, P * (t + 1))
-            acc = bank_a("acc1")
+            acc = short_bank("acc1")
             for a in range(2):
                 codes, plane = w1_q[a, b]
                 nc.tensor.matmul_mx(
@@ -248,138 +239,139 @@ def tile_list_electrolyser_slot_features_kernel(
                     rhs=v_w[a][:].bitcast(FP8X4), rhs_scale=v_s[4 * a : P, :],
                     start=(a == 0), stop=(a == 1),
                 )
-            squashed = f512("squashed")
+            squashed = work_tile("squashed")
             nc.scalar.activation(squashed[:], acc[:], ACT.Tanh)
-            gate_acc = bank_a("gate1_acc")
-            turn_back(gate_acc, gate1_t, t)
-            gain = in_slot(GAIN_SLOT[b, t], "gain", [P, S], F32) if (b, t) in GAIN_SLOT else f512("gain")
+            gate_acc = short_bank("gate1_acc")
+            turn_back(gate_acc, gate1_turned, t)
+            gain = in_slot(gain_slot, "gain", [P, S], F32) if gain_slot else work_tile("gain")
             nc.scalar.activation(gain[:], gate_acc[:], ACT.Copy, scale=g1_rows[:, b, t : t + 1])
-            nc.vector.tensor_tensor(pages[PACK * b + t][:].indirect(idx3[:]), squashed[:], gain[:], MULT)
+            nc.vector.tensor_tensor(pages[b, t][:].indirect(idx3[:]), squashed[:], gain[:], MULT)
 
         x_w = [kept("x_w%d" % b, [P, PICK], U32) for b in range(2)]
         x_s = [kept("x_s%d" % b, [P, PICK], U8) for b in range(2)]
 
-        def weave(out, planes):
-            nc.scalar.copy(
-                out.rearrange("p (c i t) -> p c t i", i=PACK, t=PACK),
-                planes.rearrange("p t (c i) -> p c t i", i=PACK),
-            )
+        def weave(copy, words, rows):
+            copy(words.rearrange("p (c i t) -> p c t i", i=PACK, t=PACK), rows.rearrange("p t (c i) -> p c t i", i=PACK))
 
-        def pick(b, t, planes, width):
-            picked = in_slot(halves[t % 2], "picked", [P, width], F32)
-            nc.vector.tensor_copy(picked[:], pages[PACK * b + t][:].indirect(idx5[:, 0 : width // 16]))
-            nc.scalar.activation(planes[:, t, 0:width], picked[:], ACT.Copy, scale=rg_rows[:, b, t : t + 1])
+        def read_slots(b, t, first, count, picked, x_rows):
+            offsets = idx5[:, first // LIST_ROWS : (first + count) // LIST_ROWS]
+            nc.vector.tensor_copy(picked, pages[b, t][:].indirect(offsets))
+            nc.scalar.activation(x_rows[:, t, first : first + count], picked, ACT.Copy, scale=rg_rows[:, b, t : t + 1])
+
+        def read_early(b, t, count, x_rows):
+            picked = in_slot(parity_slots[t % 2], "picked", [P, count], F32)
+            read_slots(b, t, 0, count, picked[:], x_rows)
 
         for a in range(2):
             w1_raw[a, 1] = load_weight("wide%d" % a, w1, PASS * a, PASS)
         w3_raw = [load_weight("wide%d" % (2 + b), w3, PASS * b, 0) for b in range(2)]
         for first_row, src in ((0, w4_scales), (4, w5_scales)):
-            for q in range(4):
+            for quad in range(QUADS):
                 nc.sync.dma_start(
-                    w45_s_raw[32 * q + first_row : 32 * q + first_row + 4, :].bitcast(I32).rearrange("r (b n) -> r b n", b=2),
-                    src[:, 4 * q : 4 * q + 4, :].bitcast(I32).rearrange("b r n -> r b n"),
+                    w45_s_raw[32 * quad + first_row : 32 * quad + first_row + 4, :].bitcast(I32).rearrange("r (b n) -> r b n", b=2),
+                    src[:, 4 * quad : 4 * quad + 4, :].bitcast(I32).rearrange("b r n -> r b n"),
                 )
 
-        planes0 = in_slot("magnitude", "planes0", [P, PACK, PICK], BF16)
-        stream1(0, 0)
-        stream1(0, 1)
+        x0_rows = in_slot("magnitude", "x0_rows", [P, PACK, PICK], BF16)
+        put_stream1(0, 0)
+        put_stream1(0, 1)
         for a in range(2):
-            w1_q[a, 1] = quantise_weight("w1_%d1" % a, w1_raw[a, 1], halves[a])
-        stream1(0, 2)
-        stream1(0, 3)
-        stream1(1, 0)
-        pick(0, 0, planes0, PICK)
-        pick(0, 1, planes0, PICK)
-        pick(0, 2, planes0, PICK)
-        pick(0, 3, planes0, PICK)
-        stream1(1, 1)
+            w1_q[a, 1] = quantise_weight("w1_%d1" % a, w1_raw[a, 1], parity_slots[a])
+        put_stream1(0, 2)
+        put_stream1(0, 3)
         w3_q = [quantise_weight("w3_%d" % b, w3_raw[b], "spare%d" % b) for b in range(2)]
         w45_s = kept("w45_s", [P, 2 * N], U8)
         nc.vector.tensor_copy(
             w45_s[:].rearrange("p (b t m) -> p b t m", b=2, t=PACK),
             w45_s_raw[:].rearrange("p (b m t) -> p b t m", b=2, t=PACK),
         )
-
+        for pair in range(2):
+            read_early(0, 2 * pair, PICK, x0_rows[:])
+            read_early(0, 2 * pair + 1, PICK, x0_rows[:])
+            put_stream1(1, pair)
         for half in range(2):
             cols = slice(PASS * half, PASS * (half + 1))
-            woven = in_slot("spare%d" % half, "woven", [P, PASS * PACK], BF16)
-            weave(woven[:], planes0[:, :, cols])
-            nc.vector.quantize_mx(x_w[0][:, cols].bitcast(FP8X4), x_s[0][:, cols], woven[:])
-        stream1(1, 2)
-        stream1(1, 3)
-        planes1 = in_slot("wide0", "planes1", [P, PACK - 1, PICK], BF16)
-        pick(1, 0, planes1, EARLY)
-        pick(1, 1, planes1, EARLY)
-        pick(1, 2, planes1, EARLY)
-        woven1 = in_slot("wide1", "woven1", [P, PICK, PACK], BF16)
-        for half in range(2):
-            cols = slice(EARLY // 2 * half, EARLY // 2 * (half + 1))
-            nc.scalar.copy(woven1[:, cols, 0 : PACK - 1], planes1[:, :, cols].rearrange("p t c -> p c t"))
+            x0_words = in_slot("spare%d" % half, "x0_words", [P, PASS * PACK], BF16)
+            weave(nc.scalar.copy, x0_words[:], x0_rows[:, :, cols])
+            nc.vector.quantize_mx(x_w[0][:, cols].bitcast(FP8X4), x_s[0][:, cols], x0_words[:])
+        put_stream1(1, 2)
+        x1_words = in_slot("wide1", "x1_words", [P, PICK, PACK], BF16)
+        x1_rows = x1_words[:].rearrange("p c t -> p t c")
+        read_early(1, 0, EARLY, x1_rows)
+        read_early(1, 1, EARLY, x1_rows)
+        put_stream1(1, 3, gain_slot="spare1")
+        read_early(1, 2, EARLY, x1_rows)
 
-        y_w = kept("y_w", [P, PICK], U32)
-        y_s = kept("y_s", [P, PICK], U8)
-        y_rows = out_0.rearrange("(p t) j -> p t j", t=PACK)
-        y_words = out_1[0].rearrange("p m i -> p (m i)").bitcast(I32)
+        def quantise_x1(first, count):
+            cols = slice(first, first + count)
+            nc.vector.quantize_mx(x_w[1][:, cols].bitcast(FP8X4), x_s[1][:, cols], x1_words[:, cols, :].rearrange("p c t -> p (c t)"))
 
-        def pick_chunk(c):
-            cols = slice(CHUNK * c, CHUNK * (c + 1))
-            offsets = idx5[:, CHUNK // 16 * c : CHUNK // 16 * (c + 1)]
-            if CHUNK * c < EARLY:
-                late = [PACK - 1]
-                picked = ring.tile([P, 1, CHUNK], F32, name="picked_chunk", align_bytes=64, bufs=4)
-            else:
-                late = list(range(PACK))
-                picked = in_slot(LATE_SLOT[c], "picked_late", [P, PACK, CHUNK], F32)
-            for n, t in enumerate(late):
-                nc.vector.tensor_copy(picked[:, n, :], pages[PACK + t][:].indirect(offsets))
-                nc.scalar.activation(woven1[:, cols, t], picked[:, n, :], ACT.Copy, scale=rg_rows[:, 1, t : t + 1])
-            nc.vector.quantize_mx(
-                x_w[1][:, cols].bitcast(FP8X4), x_s[1][:, cols], woven1[:, cols, :].rearrange("p c t -> p (c t)")
-            )
+        def read_last_slice(first, step):
+            last = PACK - 1
+            picked = ring.tile([P, CHUNK], F32, name="picked_last", align_bytes=64, bufs=EARLY // CHUNK)
+            nc.vector.tensor_copy(picked[:], pages[1, last][:].indirect(idx5[:, first // LIST_ROWS : (first + CHUNK) // LIST_ROWS]))
+            for c0 in range(0, CHUNK, step):
+                nc.scalar.activation(
+                    x1_rows[:, last, first + c0 : first + c0 + step], picked[:, c0 : c0 + step], ACT.Copy,
+                    scale=rg_rows[:, 1, last : last + 1],
+                )
+                quantise_x1(first + c0, step)
 
-        def stationary(which, b, t):
+        def read_last_chunk():
+            picked = in_slot("even", "picked_late", [P, PACK, CHUNK], F32)
+            for t in range(PACK):
+                read_slots(1, t, EARLY, CHUNK, picked[:, t, :], x1_rows)
+            quantise_x1(EARLY, CHUNK)
+
+        def stationary(weight, b, t):
             cols = slice(P * t, P * (t + 1))
             plane_cols = slice(N * b + P * t, N * b + P * (t + 1))
-            if which == 3:
+            if weight == "w3":
                 codes, plane = w3_q[b]
                 return codes[:, cols].bitcast(FP8X4), plane[:, cols]
-            if which == 4:
+            if weight == "w4":
                 return w4_w[:, b, 2 * P * t : 2 * P * (t + 1)].bitcast(FP4X4), w45_s[:, plane_cols]
             return w5_w[:, b, cols].bitcast(FP8X4), w45_s[4:P, plane_cols]
 
+        y_w = kept("y_w", [P, PICK], U32)
+        y_s = kept("y_s", [P, PICK], U8)
+        out_rows = out_0.rearrange("(p t) j -> p t j", t=PACK)
+        out_words = out_1[0].rearrange("p m i -> p (m i)").bitcast(I32)
+        tiles = PICK // P
+
         def features(jt):
             cols = slice(P * jt, P * (jt + 1))
-            acc = {which: bank_b("acc%d" % which) for which in (3, 4, 5)}
-            for b in range(2):
-                for which in (3, 4, 5):
+            acc = {"w3": short_bank("acc3"), "w4": long_bank("acc4"), "w5": long_bank("acc5")}
+            for weight in ("w3", "w4", "w5"):
+                for b in range(2):
                     for t in range(PACK):
-                        codes, plane = stationary(which, b, t)
+                        codes, plane = stationary(weight, b, t)
                         nc.tensor.matmul_mx(
-                            acc[which][:, P * t : P * (t + 1)], lhsT=codes, lhsT_scale=plane,
+                            acc[weight][:, P * t : P * (t + 1)], lhsT=codes, lhsT_scale=plane,
                             rhs=x_w[b][:, cols].bitcast(FP8X4), rhs_scale=x_s[b][:, cols],
                             start=(b == 0 and t == 0), stop=(b == 1 and t == PACK - 1),
                         )
-            y3 = in_slot(Y3_SLOT[jt], "y3", [P, S], F32) if jt in Y3_SLOT else f512("y3")
-            nc.scalar.copy(y3[:], acc[3][:])
-            product = f512("product")
-            nc.vector.tensor_tensor(product[:], acc[4][:], y3[:], MULT)
-            y = f512("y")
-            nc.vector.tensor_tensor(y[:], acc[5][:], product[:], ADD)
-            y_planes = y[:].rearrange("p (t j) -> p t j", t=PACK)
-            nc.sync.dma_start(y_rows[:, :, cols], y_planes)
-            rounded = ring.tile([P, PASS], BF16, name="y_rounded", align_bytes=64)
-            weave(rounded[:], y_planes)
-            nc.vector.quantize_mx(y_w[:, cols].bitcast(FP8X4), y_s[:, cols], rounded[:])
+            y3 = in_slot("even", "y3", [P, S], F32) if jt == 0 else work_tile("y3")
+            nc.scalar.copy(y3[:], acc["w3"][:])
+            product = work_tile("product")
+            nc.vector.tensor_tensor(product[:], acc["w4"][:], y3[:], MULT)
+            y = work_tile("y")
+            nc.vector.tensor_tensor(y[:], acc["w5"][:], product[:], ADD)
+            y_rows = y[:].rearrange("p (t j) -> p t j", t=PACK)
+            nc.sync.dma_start(out_rows[:, :, cols], y_rows)
+            y_words = ring.tile([P, PASS], BF16, name="y_words", align_bytes=64)
+            weave(nc.vector.tensor_copy if jt == tiles - 1 else nc.scalar.copy, y_words[:], y_rows)
+            nc.vector.quantize_mx(y_w[:, cols].bitcast(FP8X4), y_s[:, cols], y_words[:])
 
-        for c in range(FIRST):
-            pick_chunk(c)
-        for jt in range(PICK // P):
+        for first in range(0, EARLY, CHUNK):
+            read_last_slice(first, P if first == 0 else CHUNK)
+        for jt in range(tiles):
             features(jt)
-            if jt in AFTER:
-                pick_chunk(AFTER[jt])
+            if jt == 0:
+                read_last_chunk()
             if jt % 2 == 1:
                 cols = slice(P * (jt - 1), P * (jt + 1))
-                nc.sync.dma_start(y_words[:, cols], y_w[:, cols].bitcast(I32))
-        for q in range(4):
-            queue = nc.sync if q % 2 == 0 else nc.scalar
-            queue.dma_start(out_2[0, 4 * q : 4 * q + 4, :].bitcast(I32), y_s[32 * q : 32 * q + 4, :].bitcast(I32))
+                nc.sync.dma_start(out_words[:, cols], y_w[:, cols].bitcast(I32))
+        for quad in range(QUADS):
+            queue = nc.sync if quad % 2 == 0 else nc.scalar
+            queue.dma_start(out_2[0, 4 * quad : 4 * quad + 4, :].bitcast(I32), y_s[32 * quad : 32 * quad + 4, :].bitcast(I32))

@@ -63,6 +63,9 @@ def tile_list_electrolyser_slot_features_kernel(
 
         tab2_s = zeroed_plane("tab2_s", TC)
         w2_s = zeroed_plane("w2_s", H)
+        warm = kept("warm", [P, 2], F32)
+        nc.gpsimd.memset(warm[:], 1.0)
+        nc.scalar.activation(warm[:, 1:2], warm[:, 0:1], ACT.Sqrt)
         ident = kept("ident", [P, P], F32)
         make_identity(nc, ident[:])
         tab_s = zeroed_plane("tab_s", T)

@@ -25,7 +25,8 @@ QUADS = 4
 LIST_ROWS = 16
 CHUNK = 256
 EARLY = PICK - CHUNK
-GATES_ON_VECTOR = 2
+LAST_CHUNK_AFTER = 2
+GATES_ON_VECTOR = 1
 WORK_TILES = 12
 
 
@@ -114,13 +115,12 @@ def tile_list_electrolyser_slot_features_kernel(
         nc.sync.dma_start(w4_raw[:].bitcast(I32), w4_words.bitcast(I32).rearrange("b p n -> p b n"))
         w5_raw = in_slot("odd", "w5_raw", [P, 2, N], I32)
         nc.sync.dma_start(w5_raw[:], w5_words.rearrange("b p n i -> b p (n i)").bitcast(I32).rearrange("b p n -> p b n"))
+        idx = load_list("idx", offs)
+        load_plane(tab_s, tab_scales)
         load_page(0, 0)
         idx4 = load_list("idx4", offs4)
-        load_page(0, 1)
-        load_page(0, 2)
-        idx = load_list("idx", offs)
-        load_page(0, 3)
-        load_plane(tab_s, tab_scales)
+        for t in range(1, PACK):
+            load_page(0, t)
         tab_w = [in_slot("wide%d" % a, "tab_w%d" % a, [P, T], I32) for a in range(2)]
         for a in range(2):
             nc.sync.dma_start(tab_w[a][:], tab_words[a].rearrange("p n i -> p (n i)").bitcast(I32))
@@ -283,15 +283,10 @@ def tile_list_electrolyser_slot_features_kernel(
         put_stream1(0, 2)
         put_stream1(0, 3)
         w3_q = [quantise_weight("w3_%d" % b, w3_raw[b], "spare%d" % b) for b in range(2)]
-        w45_s = kept("w45_s", [P, 2 * N], U8)
-        nc.vector.tensor_copy(
-            w45_s[:].rearrange("p (b t m) -> p b t m", b=2, t=PACK),
-            w45_s_raw[:].rearrange("p (b m t) -> p b t m", b=2, t=PACK),
-        )
-        for pair in range(2):
-            read_early(0, 2 * pair, PICK, x0_rows[:])
-            read_early(0, 2 * pair + 1, PICK, x0_rows[:])
-            put_stream1(1, pair)
+        for t in range(2):
+            read_early(0, 2 * t, PICK, x0_rows[:])
+            read_early(0, 2 * t + 1, PICK, x0_rows[:])
+            put_stream1(1, t)
         for half in range(2):
             cols = slice(PASS * half, PASS * (half + 1))
             x0_words = in_slot("spare%d" % half, "x0_words", [P, PASS * PACK], BF16)
@@ -302,6 +297,11 @@ def tile_list_electrolyser_slot_features_kernel(
         x1_rows = x1_words[:].rearrange("p c t -> p t c")
         read_early(1, 0, EARLY, x1_rows)
         read_early(1, 1, EARLY, x1_rows)
+        w45_s = in_slot("odd", "w45_s", [P, 2 * N], U8)
+        nc.vector.tensor_copy(
+            w45_s[:].rearrange("p (b t m) -> p b t m", b=2, t=PACK),
+            w45_s_raw[:].rearrange("p (b m t) -> p b t m", b=2, t=PACK),
+        )
         put_stream1(1, 3, gain_slot="spare1")
         read_early(1, 2, EARLY, x1_rows)
 
@@ -342,7 +342,7 @@ def tile_list_electrolyser_slot_features_kernel(
         out_words = out_1[0].rearrange("p m i -> p (m i)").bitcast(I32)
         tiles = PICK // P
 
-        def features(jt):
+        def multiply(jt):
             cols = slice(P * jt, P * (jt + 1))
             acc = {"w3": short_bank("acc3"), "w4": long_bank("acc4"), "w5": long_bank("acc5")}
             for weight in ("w3", "w4", "w5"):
@@ -358,23 +358,31 @@ def tile_list_electrolyser_slot_features_kernel(
             nc.scalar.copy(y3[:], acc["w3"][:])
             product = work_tile("product")
             nc.vector.tensor_tensor(product[:], acc["w4"][:], y3[:], MULT)
+            return acc["w5"], product
+
+        def finish(jt, acc5, product):
+            cols = slice(P * jt, P * (jt + 1))
             y = work_tile("y")
-            nc.vector.tensor_tensor(y[:], acc["w5"][:], product[:], ADD)
+            nc.vector.tensor_tensor(y[:], acc5[:], product[:], ADD)
             y_rows = y[:].rearrange("p (t j) -> p t j", t=PACK)
             nc.sync.dma_start(out_rows[:, :, cols], y_rows)
             y_words = ring.tile([P, PASS], BF16, name="y_words", align_bytes=64)
             weave(nc.vector.tensor_copy if jt == tiles - 1 else nc.scalar.copy, y_words[:], y_rows)
             nc.vector.quantize_mx(y_w[:, cols].bitcast(FP8X4), y_s[:, cols], y_words[:])
+            if jt % 2 == 1:
+                two_tiles = slice(P * (jt - 1), P * (jt + 1))
+                nc.sync.dma_start(out_words[:, two_tiles], y_w[:, two_tiles].bitcast(I32))
 
         for first in range(0, EARLY, CHUNK):
             read_last_slice(first, P if first == 0 else CHUNK)
-        for jt in range(tiles):
-            features(jt)
-            if jt == 0:
+        pending = multiply(0)
+        for jt in range(1, tiles):
+            ahead = multiply(jt)
+            finish(jt - 1, *pending)
+            pending = ahead
+            if jt == LAST_CHUNK_AFTER:
                 read_last_chunk()
-            if jt % 2 == 1:
-                cols = slice(P * (jt - 1), P * (jt + 1))
-                nc.sync.dma_start(out_words[:, cols], y_w[:, cols].bitcast(I32))
+        finish(tiles - 1, *pending)
         for quad in range(QUADS):
             queue = nc.sync if quad % 2 == 0 else nc.scalar
             queue.dma_start(out_2[0, 4 * quad : 4 * quad + 4, :].bitcast(I32), y_s[32 * quad : 32 * quad + 4, :].bitcast(I32))

from contextlib import ExitStack

import concourse.mybir as mybir
from concourse.masks import make_identity

F32 = mybir.dt.float32
BF16 = mybir.dt.bfloat16
I32 = mybir.dt.int32
U32 = mybir.dt.uint32
U16 = mybir.dt.uint16
U8 = mybir.dt.uint8
FP8X4 = mybir.dt.float8_e4m3fn_x4
FP4X4 = mybir.dt.float4_e2m1fn_x4
ACT = mybir.ActivationFunctionType
MULT = mybir.AluOpType.mult
ADD = mybir.AluOpType.add

K, K2, H, N, T, TC, S, T2, PICK = 1024, 512, 1024, 512, 2048, 1024, 512, 2048, 1024
FLOPS = 2 * (K * H * S + K2 * H * S + 3 * H * N * PICK)

P = 128
PACK = 4
PASS = P * PACK
QUADS = 4
LIST_ROWS = 16
CHUNK = 256
EARLY = PICK - CHUNK
LAST_CHUNK_AFTER = 2
GATES_ON_VECTOR = 1
WORK_TILES = 12


def tile_list_electrolyser_slot_features_kernel(
    tc, tab_words, tab_scales, tab2_words, tab2_scales, offs, offs2, offs3, offs4, offs5,
    w1, g1, w2_words, w2_scales, page0, wg1, wg2, rg, w3, w4_words, w4_scales, w5_words, w5_scales,
    out_0, out_1, out_2,
):
    nc = tc.nc
    with ExitStack() as ctx:
        lists = ctx.enter_context(tc.tile_pool(name="lists", bufs=1))
        keep = ctx.enter_context(tc.tile_pool(name="keep", bufs=1))
        ring = ctx.enter_context(tc.tile_pool(name="ring", bufs=2))
        psum = ctx.enter_context(tc.psum_pool(name="psum", bufs=1))

        def kept(name, shape, dtype):
            return keep.tile(shape, dtype, name=name, align_bytes=64)

        def in_slot(slot, name, shape, dtype):
            return ring.tile(shape, dtype, name=name, tag=slot, bufs=1, align_bytes=64)

        def work_tile(name):
            return ring.tile([P, S], F32, name=name, tag="work", bufs=WORK_TILES, align_bytes=64)

        def short_bank(name):
            return psum.tile([P, S], F32, name=name, tag="short_bank", bufs=2)

        def long_bank(name):
            return psum.tile([P, S], F32, name=name, tag="long_bank", bufs=6)

        def zeroed_plane(name, width):
            plane = kept(name, [P, width], U8)
            nc.gpsimd.memset(plane[:].bitcast(I32), 0)
            return plane

        tab2_s = zeroed_plane("tab2_s", TC)
        w2_s = zeroed_plane("w2_s", H)
        warm = kept("warm", [P, 2], F32)
        nc.gpsimd.memset(warm[:], 1.0)
        nc.scalar.activation(warm[:, 1:2], warm[:, 0:1], ACT.Sqrt)
        ident = kept("ident", [P, P], F32)
        make_identity(nc, ident[:])
        tab_s = zeroed_plane("tab_s", T)
        w45_s_raw = zeroed_plane("w45_s_raw", 2 * N)

        page_rows = page0.rearrange("(b p t) c -> b t p c", b=2, t=PACK)
        pages = {(b, t): kept("page%d%d" % (b, t), [P, T2], F32) for b in range(2) for t in range(PACK)}

        def load_list(name, src):
            tile = lists.tile(list(src.shape), U16, name=name)
            nc.sync.dma_start(tile[:], src)
            return tile

        def load_page(b, t):
            nc.sync.dma_start(pages[b, t][:], page_rows[b, t])

        def load_gate(name, src):
            tile = in_slot("gate_rows", name, [P, S], F32)
            nc.sync.dma_start(tile[:], src)
            return tile

        def load_weight(slot, src, row0, col0):
            raw = in_slot(slot, "raw", [P, PACK, PASS], F32)
            nc.sync.dma_start(raw[:], src[row0 : row0 + PASS, col0 : col0 + PASS].rearrange("(p i) c -> p i c", i=PACK))
            return raw

        def load_row_gains(name, src):
            tile = kept(name, [P, 2, PACK], F32)
            nc.sync.dma_start(tile[:], src.rearrange("(b p t) -> p b t", b=2, t=PACK))
            return tile

        def load_plane(plane, src):
            rows = 4 * src.shape[0]
            for quad in range(QUADS):
                nc.sync.dma_start(plane[32 * quad : 32 * quad + rows, :].bitcast(I32), src[:, 4 * quad : 4 * quad + 4, :].bitcast(I32))

        idx2 = load_list("idx2", offs2)
        tab2_w = kept("tab2_w", [P, TC], I32)
        nc.sync.dma_start(tab2_w[:], tab2_words[0].rearrange("p n i -> p (n i)").bitcast(I32))
        wg2_rows = load_gate("wg2_rows", wg2)
        load_plane(tab2_s, tab2_scales)
        w2_w = kept("w2_w", [P, 2 * H], U8)
        nc.sync.dma_start(w2_w[:].bitcast(I32), w2_words[0].bitcast(I32))
        load_plane(w2_s, w2_scales)
        w4_raw = in_slot("even", "w4_raw", [P, 2, 2 * N], U8)
        nc.sync.dma_start(w4_raw[:].bitcast(I32), w4_words.bitcast(I32).rearrange("b p n -> p b n"))
        w5_raw = in_slot("odd", "w5_raw", [P, 2, N], I32)
        nc.sync.dma_start(w5_raw[:], w5_words.rearrange("b p n i -> b p (n i)").bitcast(I32).rearrange("b p n -> p b n"))
        idx = load_list("idx", offs)
        load_plane(tab_s, tab_scales)
        load_page(0, 0)
        idx4 = load_list("idx4", offs4)
        for t in range(1, PACK):
            load_page(0, t)
        tab_w = [in_slot("wide%d" % a, "tab_w%d" % a, [P, T], I32) for a in range(2)]
        for a in range(2):
            nc.sync.dma_start(tab_w[a][:], tab_words[a].rearrange("p n i -> p (n i)").bitcast(I32))
        w1_raw = {}
        for a in range(2):
            load_page(1, a)
            w1_raw[a, 0] = load_weight("wide%d" % (2 + a), w1, PASS * a, 0)
        load_page(1, 2)
        wg1_rows = load_gate("wg1_rows", wg1)
        g1_rows = load_row_gains("g1_rows", g1)
        idx3 = load_list("idx3", offs3)
        idx5 = load_list("idx5", offs5)
        rg_rows = load_row_gains("rg_rows", rg)
        load_page(1, 3)

        def turn_gate(rows, turned_gate):
            for jt in range(S // P):
                acc = long_bank("gate_turned")
                nc.tensor.transpose(acc[:, 0:P], rows[:, P * jt : P * (jt + 1)], ident[:])
                by_t = acc[:, 0:P].rearrange("j (u t) -> j t u", t=PACK)
                nc.scalar.copy(
                    turned_gate[:, jt].rearrange("j t (quad u) -> j t quad u", quad=QUADS),
                    by_t.unsqueeze(2).broadcast_to([P, PACK, QUADS, P // QUADS]),
                )

        def turn_back(acc, turned, t):
            for jt in range(S // P):
                nc.tensor.transpose(acc[:, P * jt : P * (jt + 1)], turned[:, jt, t, :], ident[:])

        gate2_turned = in_slot("gate_turned", "gate2_turned", [P, S // P, PACK, P], F32)
        turn_gate(wg2_rows, gate2_turned)
        gate2 = kept("gate2", [P, PACK, S], F32)

        def make_gate2(t):
            acc = long_bank("gate2_acc")
            turn_back(acc, gate2_turned, t)
            if t < GATES_ON_VECTOR:
                nc.vector.tensor_copy(gate2[:, t, :], acc[:])
            else:
                nc.scalar.copy(gate2[:, t, :], acc[:])

        v2_w = kept("v2_w", [P, S], U32)
        v2_s = kept("v2_s", [P, S], U8)
        nc.vector.tensor_copy(v2_w[:], tab2_w[:].bitcast(U32).indirect(idx2[:]))
        nc.vector.tensor_copy(v2_s[:], tab2_s[:].indirect(idx2[:]))

        w4_w = kept("w4_w", [P, 2, 2 * N], U8)
        nc.vector.tensor_copy(
            w4_w[:].rearrange("p b (t m e) -> p b t m e", t=PACK, e=2),
            w4_raw[:].rearrange("p b (m t e) -> p b t m e", t=PACK, e=2),
        )
        w5_w = kept("w5_w", [P, 2, N], I32)
        nc.vector.tensor_copy(
            w5_w[:].rearrange("p b (t m) -> p b m t", t=PACK),
            w5_raw[:].rearrange("p b (m t) -> p b m t", t=PACK),
        )

        h2 = {}
        for b in range(2):
            magnitude = in_slot("magnitude", "magnitude", [P, S // P, PACK, P], F32)
            for jt in range(S // P):
                cols = slice(P * jt, P * (jt + 1))
                acc = long_bank("acc2")
                nc.tensor.matmul_mx(
                    acc[:], lhsT=v2_w[:, cols].bitcast(FP8X4), lhsT_scale=v2_s[:, cols],
                    rhs=w2_w[:, 2 * PASS * b : 2 * PASS * (b + 1)].bitcast(FP4X4), rhs_scale=w2_s[:, PASS * b : PASS * (b + 1)],
                    start=True, stop=True,
                )
                nc.scalar.activation(magnitude[:, jt], acc[:].rearrange("j (m t) -> j t m", t=PACK), ACT.Abs)
            for t in range(PACK):
                if b == 0:
                    make_gate2(t)
                magnitude_acc = short_bank("magnitude_acc")
                turn_back(magnitude_acc, magnitude, t)
                h2[b, t] = work_tile("h2")
                nc.scalar.activation(h2[b, t][:], magnitude_acc[:], ACT.Sqrt)

        def put_stream2(b, t):
            nc.vector.tensor_tensor(pages[b, t][:].indirect(idx4[:]), h2[b, t][:], gate2[:, t, :], MULT)

        for t in range(PACK):
            put_stream2(0, t)

        v_w = [kept("v_w%d" % a, [P, S], U32) for a in range(2)]
        v_s = kept("v_s", [P, S], U8)
        for a in range(2):
            nc.vector.tensor_copy(v_w[a][:], tab_w[a][:].bitcast(U32).indirect(idx[:]))
        nc.vector.tensor_copy(v_s[:], tab_s[:].indirect(idx[:]))

        parity_slots = ("even", "odd")

        def quantise_weight(name, raw, slot):
            rounded = in_slot(slot, "rounded", [P, PASS * PACK], BF16)
            nc.scalar.copy(
                rounded[:].rearrange("p (t m i) -> p m i t", t=PACK, i=PACK),
                raw[:].rearrange("p i (m t) -> p m i t", t=PACK),
            )
            codes = kept(name + "_w", [P, PASS], U32)
            plane = kept(name + "_s", [P, PASS], U8)
            nc.vector.quantize_mx(codes[:].bitcast(FP8X4), plane[:], rounded[:])
            return codes, plane

        w1_q = {}
        for a in range(2):
            w1_q[a, 0] = quantise_weight("w1_%d0" % a, w1_raw[a, 0], parity_slots[a])
        for t in range(PACK):
            put_stream2(1, t)

        gate1_turned = in_slot("gate_turned", "gate1_turned", [P, S // P, PACK, P], F32)
        turn_gate(wg1_rows, gate1_turned)

        def put_stream1(b, t, gain_slot=None):
            cols = slice(P * t, P * (t + 1))
            acc = short_bank("acc1")
            for a in range(2):
                codes, plane = w1_q[a, b]
                nc.tensor.matmul_mx(
                    acc[:], lhsT=codes[:, cols].bitcast(FP8X4), lhsT_scale=plane[:, cols],
                    rhs=v_w[a][:].bitcast(FP8X4), rhs_scale=v_s[4 * a : P, :],
                    start=(a == 0), stop=(a == 1),
                )
            squashed = work_tile("squashed")
            nc.scalar.activation(squashed[:], acc[:], ACT.Tanh)
            gate_acc = short_bank("gate1_acc")
            turn_back(gate_acc, gate1_turned, t)
            gain = in_slot(gain_slot, "gain", [P, S], F32) if gain_slot else work_tile("gain")
            nc.scalar.activation(gain[:], gate_acc[:], ACT.Copy, scale=g1_rows[:, b, t : t + 1])
            nc.vector.tensor_tensor(pages[b, t][:].indirect(idx3[:]), squashed[:], gain[:], MULT)

        x_w = [kept("x_w%d" % b, [P, PICK], U32) for b in range(2)]
        x_s = [kept("x_s%d" % b, [P, PICK], U8) for b in range(2)]

        def weave(copy, words, rows):
            copy(words.rearrange("p (c i t) -> p c t i", i=PACK, t=PACK), rows.rearrange("p t (c i) -> p c t i", i=PACK))

        def read_slots(b, t, first, count, picked, x_rows):
            offsets = idx5[:, first // LIST_ROWS : (first + count) // LIST_ROWS]
            nc.vector.tensor_copy(picked, pages[b, t][:].indirect(offsets))
            nc.scalar.activation(x_rows[:, t, first : first + count], picked, ACT.Copy, scale=rg_rows[:, b, t : t + 1])

        def read_early(b, t, count, x_rows):
            picked = in_slot(parity_slots[t % 2], "picked", [P, count], F32)
            read_slots(b, t, 0, count, picked[:], x_rows)

        for a in range(2):
            w1_raw[a, 1] = load_weight("wide%d" % a, w1, PASS * a, PASS)
        w3_raw = [load_weight("wide%d" % (2 + b), w3, PASS * b, 0) for b in range(2)]
        for first_row, src in ((0, w4_scales), (4, w5_scales)):
            for quad in range(QUADS):
                nc.sync.dma_start(
                    w45_s_raw[32 * quad + first_row : 32 * quad + first_row + 4, :].bitcast(I32).rearrange("r (b n) -> r b n", b=2),
                    src[:, 4 * quad : 4 * quad + 4, :].bitcast(I32).rearrange("b r n -> r b n"),
                )

        x0_rows = in_slot("magnitude", "x0_rows", [P, PACK, PICK], BF16)
        put_stream1(0, 0)
        put_stream1(0, 1)
        for a in range(2):
            w1_q[a, 1] = quantise_weight("w1_%d1" % a, w1_raw[a, 1], parity_slots[a])
        put_stream1(0, 2)
        put_stream1(0, 3)
        w3_q = [quantise_weight("w3_%d" % b, w3_raw[b], "spare%d" % b) for b in range(2)]
        for t in range(2):
            read_early(0, 2 * t, PICK, x0_rows[:])
            read_early(0, 2 * t + 1, PICK, x0_rows[:])
            put_stream1(1, t)
        for half in range(2):
            cols = slice(PASS * half, PASS * (half + 1))
            x0_words = in_slot("spare%d" % half, "x0_words", [P, PASS * PACK], BF16)
            weave(nc.scalar.copy, x0_words[:], x0_rows[:, :, cols])
            nc.vector.quantize_mx(x_w[0][:, cols].bitcast(FP8X4), x_s[0][:, cols], x0_words[:])
        put_stream1(1, 2)
        x1_words = in_slot("wide1", "x1_words", [P, PICK, PACK], BF16)
        x1_rows = x1_words[:].rearrange("p c t -> p t c")
        read_early(1, 0, EARLY, x1_rows)
        read_early(1, 1, EARLY, x1_rows)
        w45_s = in_slot("odd", "w45_s", [P, 2 * N], U8)
        nc.vector.tensor_copy(
            w45_s[:].rearrange("p (b t m) -> p b t m", b=2, t=PACK),
            w45_s_raw[:].rearrange("p (b m t) -> p b t m", b=2, t=PACK),
        )
        put_stream1(1, 3, gain_slot="spare1")
        read_early(1, 2, EARLY, x1_rows)

        def quantise_x1(first, count):
            cols = slice(first, first + count)
            nc.vector.quantize_mx(x_w[1][:, cols].bitcast(FP8X4), x_s[1][:, cols], x1_words[:, cols, :].rearrange("p c t -> p (c t)"))

        def read_last_slice(first, step):
            last = PACK - 1
            picked = ring.tile([P, CHUNK], F32, name="picked_last", align_bytes=64, bufs=EARLY // CHUNK)
            nc.vector.tensor_copy(picked[:], pages[1, last][:].indirect(idx5[:, first // LIST_ROWS : (first + CHUNK) // LIST_ROWS]))
            for c0 in range(0, CHUNK, step):
                nc.scalar.activation(
                    x1_rows[:, last, first + c0 : first + c0 + step], picked[:, c0 : c0 + step], ACT.Copy,
                    scale=rg_rows[:, 1, last : last + 1],
                )
                quantise_x1(first + c0, step)

        def read_last_chunk():
            picked = in_slot("even", "picked_late", [P, PACK, CHUNK], F32)
            for t in range(PACK):
                read_slots(1, t, EARLY, CHUNK, picked[:, t, :], x1_rows)
            quantise_x1(EARLY, CHUNK)

        def stationary(weight, b, t):
            cols = slice(P * t, P * (t + 1))
            plane_cols = slice(N * b + P * t, N * b + P * (t + 1))
            if weight == "w3":
                codes, plane = w3_q[b]
                return codes[:, cols].bitcast(FP8X4), plane[:, cols]
            if weight == "w4":
                return w4_w[:, b, 2 * P * t : 2 * P * (t + 1)].bitcast(FP4X4), w45_s[:, plane_cols]
            return w5_w[:, b, cols].bitcast(FP8X4), w45_s[4:P, plane_cols]

        y_w = kept("y_w", [P, PICK], U32)
        y_s = kept("y_s", [P, PICK], U8)
        out_rows = out_0.rearrange("(p t) j -> p t j", t=PACK)
        out_words = out_1[0].rearrange("p m i -> p (m i)").bitcast(I32)
        tiles = PICK // P

        def multiply(jt):
            cols = slice(P * jt, P * (jt + 1))
            acc = {"w3": short_bank("acc3"), "w4": long_bank("acc4"), "w5": long_bank("acc5")}
            for weight in ("w3", "w4", "w5"):
                for b in range(2):
                    for t in range(PACK):
                        codes, plane = stationary(weight, b, t)
                        nc.tensor.matmul_mx(
                            acc[weight][:, P * t : P * (t + 1)], lhsT=codes, lhsT_scale=plane,
                            rhs=x_w[b][:, cols].bitcast(FP8X4), rhs_scale=x_s[b][:, cols],
                            start=(b == 0 and t == 0), stop=(b == 1 and t == PACK - 1),
                        )
            y3 = in_slot("even", "y3", [P, S], F32) if jt == 0 else work_tile("y3")
            nc.scalar.copy(y3[:], acc["w3"][:])
            product = work_tile("product")
            nc.vector.tensor_tensor(product[:], acc["w4"][:], y3[:], MULT)
            return acc["w5"], product

        def finish(jt, acc5, product):
            cols = slice(P * jt, P * (jt + 1))
            y = work_tile("y")
            nc.vector.tensor_tensor(y[:], acc5[:], product[:], ADD)
            y_rows = y[:].rearrange("p (t j) -> p t j", t=PACK)
            nc.sync.dma_start(out_rows[:, :, cols], y_rows)
            y_words = ring.tile([P, PASS], BF16, name="y_words", align_bytes=64)
            weave(nc.vector.tensor_copy if jt == tiles - 1 else nc.scalar.copy, y_words[:], y_rows)
            nc.vector.quantize_mx(y_w[:, cols].bitcast(FP8X4), y_s[:, cols], y_words[:])
            if jt % 2 == 1:
                two_tiles = slice(P * (jt - 1), P * (jt + 1))
                nc.sync.dma_start(out_words[:, two_tiles], y_w[:, two_tiles].bitcast(I32))

        for first in range(0, EARLY, CHUNK):
            read_last_slice(first, P if first == 0 else CHUNK)
        pending = multiply(0)
        for jt in range(1, tiles):
            ahead = multiply(jt)
            finish(jt - 1, *pending)
            pending = ahead
            if jt == LAST_CHUNK_AFTER:
                read_last_chunk()
        finish(tiles - 1, *pending)
        for quad in range(QUADS):
            queue = nc.sync if quad % 2 == 0 else nc.scalar
            queue.dma_start(out_2[0, 4 * quad : 4 * quad + 4, :].bitcast(I32), y_s[32 * quad : 32 * quad + 4, :].bitcast(I32))
